import numpy as np, ml_dtypes
CORES = [1,5,17,21,33,37,49,53]
N = 8
import mx_ref
BF = ml_dtypes.bfloat16
def gentries(a):
    return np.ascontiguousarray(a.reshape(8, 16, -1).transpose(0, 2, 1)).reshape(8, -1)
def gtable(e):
    e = np.asarray(e); return np.ascontiguousarray(e.reshape(8, -1, 16).transpose(0, 2, 1)).reshape(128, -1).astype(np.int32)
def gcols(t, e):
    v = np.concatenate([t.reshape(8, 16, -1, 4), np.zeros((8, 16, 1, 4), BF)], axis=2)
    return np.ascontiguousarray(np.stack([v[g][:, e[g]] for g in range(8)])).reshape(128, -1)
def tile(rs):
    return np.stack(rs, axis=2).reshape(128, -1).astype(BF)
def pick(q, e):
    c = np.concatenate([q[0].reshape(128, -1, 4), np.zeros((128, 1, 4), np.uint8)], axis=1); s = np.concatenate([q[1], np.ones((16, 1), np.uint8)], axis=1)
    return (np.ascontiguousarray(c[:, e].reshape(128, -1)), np.ascontiguousarray(s[:, e]))
def join(*qs):
    return (np.concatenate([q[0] for q in qs], axis=1), np.concatenate([q[1] for q in qs], axis=1))
def put(q, e, v):
    c, s = q[0].reshape(128, -1, 4).copy(), q[1].copy(); c[:, e] = v[0].reshape(128, -1, 4); s[:, e] = v[1]
    return (c.reshape(128, -1), s)
def pk(c, s):
    return (np.ascontiguousarray(c), mx_ref.live(s))
def emit(q):
    return q[0], q[1]
def packed(v, rng):
    q = [mx_ref.quantize(np.ascontiguousarray(v[r])) for r in range(N)]
    return np.stack([a for a, b in q]), np.stack([mx_ref.plane(b, rng) for a, b in q])
def values_of_codes():
    e, c = np.zeros((128, 128, 4), np.float32), np.zeros((128, 2, 4), np.uint8)
    e[np.arange(128), np.arange(128), 0] = 1
    c[:127, :, 0] = np.arange(256).reshape(2, 128).T[:127]
    return mx_ref.matmul(mx_ref.quantize(e.reshape(128, 512).astype(BF)), (c.reshape(128, 8), np.full((16, 2), 127, np.uint8))).T.reshape(-1).astype(np.float64)
CODE_VALUE, SCALE_VALUE = values_of_codes(), 2.0 ** (np.arange(256) - 127.0)
def decode(q):
    return (CODE_VALUE[q[0]].reshape(16, 8, -1, 4) * SCALE_VALUE[q[1]][:, None, :, None] + 0.0).reshape(128, -1).astype(np.float32)
def f(rng, *shape):
    return mx_ref.flush((rng.standard_normal(shape, dtype=np.float32) * np.exp2(rng.integers(-2, 3, shape[:-1] + (1,)))).astype(BF))
def wide(rng, *shape, cols=0):
    v = rng.standard_normal(shape, dtype=np.float32) * np.exp2(rng.integers(-12, 13, shape)).astype(np.float32)
    if cols: v *= np.repeat(np.exp2(rng.integers(-cols, cols + 1, shape[:-2] + (1, shape[-1] // 4))) * (rng.random(shape[:-2] + (1, shape[-1] // 4)) > 0.0625), 4, axis=-1).astype(np.float32)
    return mx_ref.flush(v.astype(BF))
C = 320
STEP = [1, 2, 4]
def take(a, e):
    return np.take_along_axis(a, e, axis=-1)
def effective(back):
    e = np.ones(back.shape, bool)
    for j in range(C - 1, -1, -1):
        up = back[..., j]
        e[..., j] = (up <= j) | ~take(e, up[..., None])[..., 0]
    return e
def numbers_of(rng):
    return {"x": np.array(f(rng, N, 128, 4 * C)), "u": np.array(f(rng, N, 128, 512)), "v": np.array(f(rng, N, 128, 512))}
def stored(back, ring, mate):
    return {k: np.stack([gtable(e[r]) for r in range(N)]) for k, e in (("ud", np.argsort(back, axis=-1)), ("iv", back), ("hp", ring), ("mt", mate))}
def shuffled(rng):
    return rng.permuted(np.tile(np.arange(C), (N, 8, 1)), axis=2)
def linked(order):
    e = np.zeros_like(order)
    np.put_along_axis(e, order, np.roll(order, -1, axis=-1), axis=-1)
    return e
def mates(rng):
    a = shuffled(rng)
    e = np.zeros_like(a)
    np.put_along_axis(e, a[..., ::2], a[..., 1::2], axis=-1)
    np.put_along_axis(e, a[..., 1::2], a[..., ::2], axis=-1)
    return e
def runs(rng, back):
    return linked(np.argsort(effective(back) + rng.random(back.shape), axis=-1))
def lists(rng):
    return stored(shuffled(rng), linked(shuffled(rng)), mates(rng))
def layers(rng, still=()):
    w = np.array(f(rng, N, 128, 2048)).reshape(N, 8, 16, 4, 8, 16, 4)
    for i in still:
        w[:, :, i] = 0
        w[:, :, :, :, :, i] = 0
    return w
def weights(rng, w):
    c, s = packed(np.ascontiguousarray(w).reshape(N, 128, 2048), rng)
    return {"wc": c, "ws": s}
def setup_inputs(rng):
    return {**numbers_of(rng), **lists(rng), **weights(rng, layers(rng))}
def setup_inputs_ties(rng):
    d = numbers_of(rng)
    o = rng.permutation(N)
    k = rng.choice([-1.0, 0.0, 1.0, 1.0], (N, 8, C))
    k[o[0]] = 0
    k[o[1]] = 1
    k[o[2]] = (rng.permutation(8) % 2 * 2.0 - 1.0)[:, None]
    x = d["x"].reshape(N, 8, 16, C, 4)
    x[:, :, 0] = 0
    x[:, :, 0, :, 0] = k.astype(np.float32).astype(BF)
    u = d["u"].reshape(N, 128, 128, 4)
    u[:, :, ::16] = 0
    for h in range(0, 128, 16): u[:, h, h, 0] = 1
    back = np.zeros((N, 8, C), np.int64)
    for r in range(N):
        for g, m in enumerate(rng.permutation([1, 1, 1, 2, 2, 3, C // 8, 0])):
            a = rng.integers(0, m, C) if m else np.arange(C)
            for i in np.unique(a):
                e = np.flatnonzero(a == i)
                back[r, g, e] = np.roll(e, -1)
    mate = mates(rng)
    tau = np.where((k > 0) & (take(k, mate) > 0), mate, np.arange(C))
    return {"x": x.reshape(N, 128, 4 * C), "u": u.reshape(N, 128, 512), "v": d["v"], **stored(take(tau, back), runs(rng, back), mate), **weights(rng, layers(rng, [0]))}
def setup_inputs_near(rng):
    d = numbers_of(rng)
    i = np.arange(N)
    first = np.minimum(i, i ^ STEP[0])
    small = np.isin(first, rng.permutation(np.unique(first))[:N // 4])
    k = np.where(small, 2.0 ** -30, 1.0)
    x = d["x"].astype(np.float32).reshape(N, 8, 16, C, 4)
    x[:, :, :8] = 0
    s = rng.choice([-1.0, 0.0, 1.0, 1.0], (N, 8, C)) * k[:, None, None]
    x[:, :, 0, :, 0] = 1.125 * s
    x[:, :, 1, :, 0] = -1.25 * s
    x[:, :, 3, :, 0] = np.where(small[:, None, None], rng.choice([-1.0, 1.0], (N, 8, C)) * 2.0 ** -30, 0.0)
    x[:, :, 4, :, 0] = np.where(small, 2.0 ** -27, 0.0)[:, None, None]
    u = d["u"].reshape(N, 128, 128, 4)
    u[:, :, ::16] = 0
    w = layers(rng, range(8))
    for r in range(N):
        at = [0, C - 1, int(rng.integers(C)), int(rng.integers(C))]
        for g, j in zip(rng.permutation(8)[:4], at): x[r, g, 0, j, 0] = 2.0 ** 30 * rng.choice([-1.0, 1.0])
        for g in range(8):
            h = 16 * g
            u[r, h, h, 0] = 1.125 * k[r]
            u[r, h + 1, h, 0] = k[r]
            u[r, h + 2, h, 0] = 1.125 * k[r]
            u[r, h + 5, h, 0] = k[r]
            if small[r]:
                w[r, g, 3, 0, g, 2, 0] = 2.0 ** -7
                w[r, g, 3, 0, g, 5, 0] = -2.0 ** -7
    return {"x": x.reshape(N, 128, 4 * C).astype(BF), "u": u.reshape(N, 128, 512), "v": d["v"], **lists(rng), **weights(rng, w)}
def setup_inputs_odd(rng):
    d = numbers_of(rng)
    x = (1.0 + (2 * rng.integers(0, 64, (N, 16, 8, C, 4)) + 1) * 2.0 ** -7) * np.exp2(-rng.integers(0, 7, (N, 16, 8, C, 4)).astype(np.float64)) * rng.choice([-1.0, 1.0], (N, 16, 8, C, 4))
    x[:, ::2] = 0
    x[:, :, 0, :, 0] = 1.96875 * 2.0 ** 8 * rng.choice([-1.0, 1.0], (N, 16, C))
    x[:, ::2, 1, :, 0] = (1.0 + 0.125 * (rng.random((N, 8, C)) < 0.75)) * 2.0 ** -5
    x[:, ::2, 2, :, 0] = (1.0 + 0.125 * (rng.random((N, 8, C)) < 0.25)) * 2.0 ** -5
    x[:, 14, 0, :, 1] = 16.0
    u = d["u"].reshape(N, 128, 128, 4)
    u[:, :, ::16] = 0
    for h in range(0, 128, 16):
        u[:, h + 1, h, 0] = 1
        u[:, h + 2, h, 0] = -1
        u[:, h + 3, h, 0] = 1
    w = layers(rng, [0, 1, 2, 8])
    w[:, 7, 0, 0, :, 0, 1] = -16.0
    return {"x": x.astype(np.float32).reshape(N, 128, 4 * C).astype(BF), "u": u.reshape(N, 128, 512), "v": d["v"], **lists(rng), **weights(rng, w)}
def setup_inputs_ends(rng):
    d = numbers_of(rng)
    x = np.zeros((N, 8, 16, C, 4))
    u = d["u"].astype(np.float32).reshape(N, 128, 128, 4)
    v = d["v"].astype(np.float32)
    w = np.zeros((N, 128, 4, 128, 4), np.float32)
    o, kinds = np.zeros(N, np.int64), rng.permutation(4)
    left = rng.permutation(np.unique(np.minimum(np.arange(N), np.arange(N) ^ STEP[0])))
    o[left] = kinds[:N // 2]
    o[left ^ STEP[0]] = kinds[(np.arange(N // 2) + 2) % 4]
    i, j = np.arange(128), np.arange(C)
    turns = np.stack([j ^ 1, C - 1 - j, (j + C // 2) % C])
    ways = np.stack([np.roll(j, -1), j, C - 1 - j, np.roll(j, 1)])
    mate = np.stack([turns[rng.permutation(8) % 3] for r in range(N)])
    plan = np.stack([ways[rng.permutation(8) % 4] for r in range(N)])
    ring, back = runs(rng, plan), plan.copy()
    for r in range(N):
        h = rng.permutation(8)
        sign = np.where(h < 2, 0.0, h % 2 * 2.0 - 1.0)
        c = sign[None, :, None]
        e = rng.permutation(8)
        ring[r, e[:2]] = np.roll(j, -1)
        ring[r, e[2:4]] = np.roll(j, 1)
        if o[r] in (0, 2): back[r, sign < 0] = take(mate[r], plan[r])[sign < 0]
        low = -(0.9 + 0.1 * rng.random((8, 16, C, 4))) * 2.0 ** 30
        if o[r] == 0: x[r] = low
        if o[r] == 1: x[r] = np.where((rng.random(C) < 0.5)[:, None], (1.0 + 0.4 * rng.random((8, 16, C, 4))) * 2.0 ** 27, low)
        if o[r] == 2: x[r] = -(1.0 + 0.125 * rng.integers(0, 8, (8, 16, C, 4))) * 2.0 ** -30
        if o[r] == 3: x[r] = d["x"][r].astype(np.float32).reshape(8, 16, C, 4)[:, :, :1]
        if o[r] < 2:
            x[r, 7, 15, :, 3] *= 2.0 ** -6
            u[r, :, ::16] = c * (0.9 + 0.1 * rng.random((128, 8, 4))) * 2.0 ** 30
            v[r] = rng.choice([-1.0, 1.0], (128, 512)) * (0.9 + 0.1 * rng.random((128, 512))) * 2.0 ** 30
        if o[r] == 2:
            u[r, :, ::16] = c * (1.0 + 0.125 * rng.integers(0, 8, (128, 8, 4))) * 2.0 ** -30
            v[r] = rng.choice([-1.0, 1.0], (128, 512)) * (1.0 + 0.125 * rng.integers(0, 8, (128, 512))) * 2.0 ** -30
        if o[r] == 3: u[r, :, ::16] *= np.abs(c).astype(np.float32)
        k = np.array([8.0, 16.0, 32.0])[rng.permutation(8) % 3]
        for b in range(4): w[r, i, b, i, b] = k[i // 16]
        if o[r] == 2:
            w[r, 127, 3, 127, 3] = 256.0
            w[r, 126, 3, 126, 3] = 2.0 ** -8
    return {"x": x.astype(np.float32).reshape(N, 128, 4 * C).astype(BF), "u": u.reshape(N, 128, 512).astype(BF), "v": v.astype(BF), **stored(back, ring, mate), **weights(rng, w.astype(BF))}
def setup_inputs_spread(rng):
    d = setup_inputs(rng)
    d["x"] = wide(rng, N, 128, 4 * C, cols=6)
    return d
def check_inputs(d):
    b = []
    for k in ("x", "u", "v"):
        a = np.abs(d[k].astype(np.float32))
        if not (np.isfinite(a).all() and ((a == 0) | (a >= 2.0 ** -30) & (a <= 2.0 ** 30)).all()): b.append("a value of " + k)
    none, least, most = [emit(mx_ref.quantize(np.full((128, 16), k, np.float32).astype(BF)))[1][0, 0] for k in (0.0, 2.0 ** -8, 2.0 ** 8)]
    own = np.arange(C)
    for r in range(N):
        ud, iv, hp, mt = [gentries(d[k][r]) for k in ("ud", "iv", "hp", "mt")]
        if any(((a < 0) | (a >= C)).any() for a in (ud, iv, hp, mt)): b.append("an entry of a list")
        else:
            if (np.sort(ud, axis=1) != own).any(): b.append("ud: a permutation")
            if (take(ud, iv) != own).any(): b.append("iv: the inverse of ud")
            if (take(mt, mt) != own).any() or (mt == own).any(): b.append("mt: pairs of columns")
            at, seen = np.zeros((8, 1), np.int64), np.zeros((8, C), bool)
            for j in range(C):
                at = take(hp, at)
                np.put_along_axis(seen, at, True, axis=1)
            if not seen.all(): b.append("hp: a ring")
        if ((d["wc"][r] == 0x7F) | (d["wc"][r] == 0xFF)).any(): b.append("wc: a code that is no number")
        s = mx_ref.live(d["ws"][r])
        if ((s != none) & ((s < least) | (s > most))).any(): b.append("ws: a scale out of range")
    return b
def halfsum(s, t):
    return ((s.astype(np.float32) + t.astype(np.float32)) * np.float32(0.5)).astype(BF)
def reference(x, u, v, ud, iv, hp, mt, wc, ws):
    qu = [mx_ref.quantize(u[r]) for r in range(N)]
    lay = [pk(wc[r], ws[r]) for r in range(N)]
    to, back, ring, mate = [[gentries(a[r]) for r in range(N)] for a in (ud, iv, hp, mt)]
    now = [x[r] for r in range(N)]
    for step in STEP:
        t, past, sent = [], [], []
        for r in range(N):
            q = mx_ref.quantize(now[r])
            s = mx_ref.matmul(qu[r], q)[::16] > 0
            t.append(decode(q).astype(BF))
            tau = np.where(s & take(s, mate[r]), mate[r], np.arange(C))
            to[r], back[r] = take(to[r], tau), take(tau, back[r])
            e, b = effective(back[r]), ring[r]
            while not take(e, b).all(): b = np.where(take(e, b), b, take(ring[r], b))
            past.append(b)
            sent.append(mx_ref.quantize(halfsum(gcols(t[r], b), gcols(t[r], back[r]))))
        for r in range(N):
            p = r ^ step
            h = tile([mx_ref.matmul(pick(lay[r], np.arange(128 * b, 128 * b + 128)), sent[p]) * np.float32(0.03125) for b in range(4)])
            now[r] = halfsum(gcols(t[r], to[r]), gcols(h, take(past[p], back[r])))
    y, uo = np.zeros((N, 128, C), np.float32), np.zeros((N, 8, C), np.float32)
    oc, osc = np.zeros((N, 128, 4 * C), np.uint8), np.zeros((N, 16, C), np.uint8)
    for r in range(N):
        q = mx_ref.quantize(now[r])
        y[r] = mx_ref.matmul(mx_ref.quantize(v[r]), q)
        uo[r] = to[r]
        oc[r], osc[r] = emit(q)
    return {"y": y, "uo": uo, "oc": oc, "osc": osc}

@@ -1,0 +1,519 @@
+from concourse.bass import DstId, RemoteDMATransfer
+from concourse.mybir import dt, AluOpType as A, ActivationFunctionType as F
+
+C = 320
+RAD = [4, 4, 4, 5]
+SIZES = [4, 16, 64, 320]
+STEP = [1, 2, 4]
+PADZ = 16
+BIG, LOW = 1024.0, -8192.0
+BIGS, LOWS = 4.0, -64.0
+FRAC = 1.0 / 1024.0
+F4, U8, BF, F32, I32, U16 = "float8_e4m3fn_x4", "uint8", "bfloat16", "float32", "int32", "uint16"
+
+SCRATCH = {}
+SEMAPHORES = ["qv", "qs", "qt", "qg", "sent"]
+
+
+def _buf(name, n, dtype):
+    SCRATCH[name] = ("sbuf", [128, n], dtype)
+
+
+for _n in ("ud", "iv", "hp", "mt"):
+    _buf(_n + "in", 20, I32)
+    _buf(_n + "o", 20, U16)
+    SEMAPHORES.append("d" + _n)
+for _n in ("x", "u", "v", "wc", "ws", "y0", "y1", "oc", "s0", "s1", "s2", "s3", "uo"):
+    SEMAPHORES.append("d" + _n)
+for _n, _w, _t in (("xin", 1280, BF), ("uin", 512, BF), ("vin", 512, BF), ("eb", 520, BF), ("ones", 520, BF),
+                   ("iotj", C, F32), ("iotc", 328, F32), ("ti", 16, I32), ("c16", 20, I32), ("pa", 20, I32), ("po", 20, U16), ("m16", 32, F32),
+                   ("msk", C, F32), ("msks", C, BF),
+                   ("pf", 2, F32), ("bigc", 2, F32), ("bigs", 2, F32), ("eif", 20, F32), ("kk", 80, F32),
+                   ("mtw", C, F32), ("ivmw", C, F32), ("xa", C, F32), ("xb", C, F32),
+                   ("fa", 2 * C, F32), ("fb", 2 * C, F32), ("sg", C, F32), ("rsc", C, F32), ("rofs", 20, U16), ("wl", 16, F32), ("lo", 2, U16),
+                   ("lci", 4, I32), ("lc", 4, F32), ("ro", 20, U16), ("pw", C, F32), ("km", C, F32), ("pmo", 20, U16), ("rw", 328, F32), ("wd", C, F32), ("ordo", 20, U16),
+                   ("da", C, F32), ("dd", C, F32), ("tt", C, F32), ("sc", C, F32), ("scs", C, BF), ("t1", 20, F32),
+                   ("ivs", 20, F32), ("ivd", 20, F32), ("uds", 20, F32), ("udd", 20, F32), ("sf", 20, F32), ("sm", 20, F32), ("sn", 20, F32),
+                   ("xle", 20, F32), ("xao", 20, U16), ("xbo", 20, U16), ("oa", 22, U16), ("ob", 22, U16),
+                   ("pp", C, BF), ("sw", C, BF), ("giv", C, BF), ("vi", C, I32), ("st", C, F32), ("bw", C, F32), ("ew", C, F32), ("sce", C, F32),
+                   ("th", 1280, BF), ("thp", 1280, BF), ("tiv", 1280, BF), ("tu", 1280, BF), ("hh", 1280, BF), ("xt", 1280, BF), ("zt", 1280, BF),
+                   ("uof", 8, U16), ("ys", C, F32),
+                   ("qu", 128, F4), ("su", 128, U8), ("qr", 128, F4), ("sr", 128, U8), ("qv_", 128, F4), ("sv", 128, U8),
+                   ("qw", 512, F4), ("sw_", 512, U8), ("qe", 512, F4), ("se", 512, U8), ("qz", C, F4), ("sz", C, U8), ("udn", 20, U16)):
+    _buf(_n, _w, _t)
+for _n in ("ivn", "ivp", "bn", "bp", "en", "ep"):
+    _buf(_n, 72, U16)
+for _i in range(4):
+    _buf("d%d" % _i, 16 + C, F32)
+    _buf("qx%d" % _i, C, F4)
+    _buf("sx%d" % _i, C, U8)
+for _i in range(3):
+    _buf("qp%d" % _i, C, F4)
+    _buf("sp%d" % _i, C, U8)
+    SEMAPHORES += ["%s%d" % (_n, _i) for _n in ("aq", "as", "ai", "ab", "ae")]
+for _i in range(8):
+    SCRATCH["ps%d" % _i] = ("psum", [128, 512], F32)
+
+
+def rank_program(g, core, T, topo):
+    rank = T.rank_of(core)
+    if rank is None:
+        return
+    V, S, P, Y = g.vector, g.scalar, g.tensor, g.sync
+    eng = {"v": V, "s": S, "t": P, "g": g, "y": Y}
+    count = {"qv": 0, "qs": 0, "qt": 0, "qg": 0}
+    seen = {q: {} for q in eng}
+    lastw, readers = {}, {}
+    total = {}
+
+    def need(q, rd, wr):
+        dep = {}
+        for k in rd:
+            for s, n in lastw.get(k, ()):
+                dep[s] = max(dep.get(s, 0), n)
+        for k in wr:
+            for s, n in list(lastw.get(k, ())) + readers.get(k, []):
+                dep[s] = max(dep.get(s, 0), n)
+        for s, n in dep.items():
+            if seen[q].get(s, 0) < n:
+                eng[q].wait_ge(T.sem[s], n)
+                seen[q][s] = n
+
+    def note(tok, rd, wr):
+        for k in rd:
+            readers.setdefault(k, []).append(tok)
+        for k in wr:
+            lastw[k] = [tok]
+            readers[k] = []
+
+    rec, free, fin = [None], {q: 0.0 for q in eng}, {}
+    usual = {"copy": 0.1, "tt": 0.65, "ts": 0.1, "scan": 0.35, "set": 0.08, "quant": 0.2, "act": 0.6, "mm": 0.35, "iota": 0.8, "sel": 1.2}
+    small = ("t1", "sf", "sm", "sn", "ivs", "ivd", "uds", "udd", "xle")
+    quarter = [("sc", i) for i in range(5)] + [("d%d" % s, i) for s in range(4) for i in range(5)]
+
+    def start(q, rd, wr):
+        t = free[q]
+        for k in rd:
+            for x in lastw.get(k, ()):
+                t = max(t, fin.get(x, 0.0) + 0.06)
+        for k in wr:
+            for x in list(lastw.get(k, ())) + readers.get(k, []):
+                t = max(t, fin.get(x, 0.0) + 0.06)
+        return t
+
+    def lasts(name, wr):
+        if name == "tt" and wr[0] in small:
+            return 0.1
+        if wr and (wr[0] in quarter or wr[0] == "wl"):
+            return 0.2 if name == "tt" else 0.12
+        return usual[name]
+
+    def merge(*chains):
+        chains, done = [list(c) for c in chains], set()
+        while any(chains):
+            best = None
+            for c in chains:
+                while c and c[0][0] == "mark":
+                    done.add(c.pop(0)[1])
+                if c and c[0][0] == "after":
+                    if c[0][1] not in done:
+                        continue
+                    c.pop(0)
+                if c:
+                    f, a = c[0]
+                    t = start(a[0], a[2], a[3]) if f is op else (start(a[0], a[2], []) if f is dma else 0.0)
+                    if best is None or t < best[0] - 1e-6:
+                        best = (t, c)
+            if best is None:
+                continue
+            f, a = best[1].pop(0)
+            f(*a[:-1], **a[-1])
+
+    def chain(*parts):
+        out = []
+        for p in parts:
+            if isinstance(p, tuple):
+                out.append(p)
+                continue
+            rec[0] = out
+            for _ in p:
+                pass
+            rec[0] = None
+        return out
+
+    def op(q, name, rd, wr, *a, **kw):
+        if rec[0] is not None:
+            rec[0].append((op, (q, name, rd, wr) + a + (kw,)))
+            return
+        t = start(q, rd, wr)
+        free[q] = t + lasts(name, wr)
+        fin[("q" + q, count["q" + q] + 1)] = free[q]
+        need(q, rd, wr)
+        f = {"copy": V.tensor_copy, "tt": V.tensor_tensor, "ts": V.tensor_scalar, "scan": V.tensor_tensor_scan, "set": V.memset,
+             "quant": V.quantize_mx, "act": S.activation, "mm": P.matmul_mx, "iota": g.iota, "sel": g.affine_select}[name]
+        s = "q" + q
+        count[s] += 1
+        f(*a, **kw).then_inc(T.sem[s], 1)
+        total[s] = count[s]
+        note((s, count[s]), rd, wr)
+
+    def dma(q, sem, rd, wr, out, in_):
+        need(q, rd, wr)
+        total[sem] = total.get(sem, 0) + 16
+        free[q] += 0.06
+        fin[(sem, total[sem])] = free[q] + (3.5 if sem == "dx" else 2.2)
+        eng[q].dma_start(out, in_).then_inc(T.sem[sem], 16)
+        note((sem, total[sem]), rd, wr)
+
+    def send(p, key, out, in_, sem):
+        if rec[0] is not None:
+            rec[0].append((send, (p, key, out, in_, sem, {})))
+            return
+        need("g", [key], [])
+        dst = T.cores[p]
+        rid, pid = topo.addr(dst)[:2]
+        e = topo.engines(core, dst)[:8]
+        total["sent"] = total.get("sent", 0) + len(e)
+        g.remote_dma(out, in_, T.sem[sem], T.sem.sent, pid, rid, sum(1 << i for i in e))
+
+    def lands(key, sem, p):
+        n = len(topo.engines(T.cores[p], core)[:8])
+        lastw[key] = [(sem, n)]
+        fin[(sem, n)] = 14.0
+        total[sem] = n
+
+    for r in range(3):
+        p = rank ^ STEP[r]
+        for k, s in (("qp", "aq"), ("sp", "as"), ("ivp", "ai"), ("bp", "ab"), ("ep", "ae")):
+            lands("%s%d" % (k, r), "%s%d" % (s, r), p)
+
+    def li(name, lo=0, hi=20):
+        if name[:-1] in ("ivn", "ivp", "bn", "bp", "en", "ep"):
+            o = 24 * int(name[-1])
+            return T[name[:-1]][:, o + lo:o + hi]
+        return T[name][:, lo:hi]
+
+    dma("y", "dhp", [], ["hpin"], T.hpin[:], T.hp[:])
+    dma("s", "div", [], ["ivin"], T.ivin[:], T.iv[:])
+    dma("y", "dx", [], ["xin"], T.xin[:], T.x[:])
+    dma("s", "dmt", [], ["mtin"], T.mtin[:], T.mt[:])
+    dma("y", "du", [], ["uin"], T.uin[:], T.u[:])
+    dma("s", "dud", [], ["udin"], T.udin[:], T.ud[:])
+    dma("y", "dws", [], ["sw_"], T.sw_[:], T.ws[:])
+    dma("y", "dwc", [], ["qw"], T.qw[:].bitcast(dt.uint8), T.wc[:])
+    dma("y", "dv", [], ["vin"], T.vin[:], T.v[:])
+
+    op("g", "iota", [], ["iotj"], T.iotj[:], [[1, C]], 0, 0, allow_small_or_imprecise_dtypes=True)
+    op("g", "iota", [], ["ti"], T.ti[:], [[1, 16]], 128, -1)
+    op("g", "iota", [], ["pa"], T.pa[:], [[0, 20]], 0, 1)
+    op("g", "iota", [], ["c16"], T.c16[:], [[16, 20]], 0, 0)
+    op("v", "set", [], ["ones"], T.ones[:], 1.0)
+    op("g", "sel", ["ones"], ["eb"], T.eb[:], T.ones[:], [[1, 520]], A.is_equal, 0.0, -3, -4)
+    op("g", "iota", [], ["km"], T.km[:], [[1, C]], -1, 0, allow_small_or_imprecise_dtypes=True)
+    op("v", "set", [], ["iotc2"], T.iotc[:, C:C + 8], float(C))
+    op("v", "set", [], ["rw2"], T.rw[:, C:C + 8], float(C - 1))
+    op("s", "act", ["iotj"], ["iotc"], T.iotc[:, 0:C], T.iotj[:], F.Copy, bias=FRAC)
+    for n in ("hp", "iv", "mt"):
+        op("v", "copy", [n + "in"], [n + "o"], T[n + "o"][:], T[n + "in"][:])
+    op("s", "act", ["iotj", "hpo"], ["fa"], T.fa[:, 0:C], T.iotj[:].indirect(T.hpo[:]), F.Copy)
+    op("s", "act", ["iotj", "mto"], ["mtw"], T.mtw[:], T.iotj[:].indirect(T.mto[:]), F.Copy)
+    op("v", "ts", ["ti"], ["ti"], T.ti[:], T.ti[:], 15, None, A.bitwise_and)
+    op("v", "ts", ["pa"], ["pa"], T.pa[:], T.pa[:], 15, None, A.bitwise_and)
+    op("v", "copy", ["pa"], ["po"], T.po[:], T.pa[:])
+    op("v", "ts", ["ti"], ["sce"], T.sce[:, 0:16], T.ti[:], 0.0, LOW, A.is_equal, A.mult)
+    op("v", "ts", ["ti"], ["ew"], T.ew[:, 0:16], T.ti[:], 1.0, BIG, A.is_equal, A.mult)
+    op("v", "tt", ["sce", "ew"], ["m16"], T.m16[:, 0:16], T.sce[:, 0:16], T.ew[:, 0:16], A.add)
+    op("s", "act", ["m16", "po"], ["msk"], T.msk[:], T.m16[:, 0:16].indirect(T.po[:]), F.Copy)
+    op("v", "ts", ["m16"], ["m16s"], T.m16[:, 16:32], T.m16[:, 0:16], BIGS / BIG, LOWS, A.mult, A.max)
+    op("s", "act", ["m16s", "po"], ["msks"], T.msks[:], T.m16[:, 16:32].indirect(T.po[:]), F.Copy)
+    op("v", "copy", ["pa"], ["pf"], T.pf[:], T.pa[:, 0:2])
+    op("v", "ts", ["pa"], ["bigc"], T.bigc[:], T.pa[:, 0:2], 15.0, BIG, A.is_lt, A.mult)
+
+    def places():
+        op("v", "ts", ["c16", "pf"], ["eif"], T.eif[:], T.c16[:], T.pf[:, 0:1], None, A.add); yield
+        op("v", "copy", ["ivin"], ["ivs"], T.ivs[:], T.ivin[:]); yield
+
+    def places2():
+        for i in range(4):
+            op("v", "set", [], [("d%d" % i, -1)], T["d%d" % i][:, 0:PADZ], 0.0); yield
+        op("v", "ts", ["pa"], ["bigs"], T.bigs[:], T.pa[:, 0:2], 15.0, BIGS, A.is_lt, A.mult); yield
+        for i in range(4):
+            nb = C // SIZES[i]
+            op("v", "ts", ["eif"], ["k%d" % i], T.kk[:, 20 * i:20 * i + 20], T.eif[:], -1.0 / nb, -(PADZ + 0.25) / nb, A.mult, A.add); yield
+        op("v", "ts", ["k0", "k1", "k2", "k3", "bigc"], ["k0", "k1", "k2", "k3"], T.kk[:], T.kk[:], T.bigc[:, 0:1], None, A.subtract); yield
+
+    def scan(dst, src, rd, lo=0):
+        op("v", "scan", rd + ["msk"], [dst], T[dst][:], T.msk[:], src, 0.0, A.add, A.max)
+
+    def ring():
+        for n in ("fa", "fb"):
+            op("s", "act", ["iotj"], [n + "i"], T[n][:, C:2 * C], T.iotj[:], F.Copy)
+        op("v", "set", [], ["lo"], T.lo[:], float(C - 1)); yield
+        for k in range(4):
+            op("v", "ts", ["pa"], [("lci", k)], T.lci[:, k:k + 1], T.pa[:, 0:1], k, 1, A.logical_shift_right, A.bitwise_and); yield
+        op("v", "ts", [("lci", k) for k in range(4)] + ["bigc"], ["lc"], T.lc[:], T.lci[:], float(C), T.bigc[:, 0:1], A.mult, A.subtract); yield
+        cur, nxt, off = "fa", "fb", "hpo"
+
+        def part(src, keys_, n, outs):
+            op("v", "scan", keys_ + ["msk"], ["rsc"], T.rsc[:, 0:n], T.msk[:, 0:n], src, 0.0, A.add, A.max); yield
+            for k, o, c in outs:
+                op("v", "ts", ["rsc", "lc", "bigc"], [k], o, T.rsc[:, 15:n:16], c[0], None, c[1]); yield
+
+        minus = (T.bigc[:, 0:1], A.subtract)
+        op("s", "act", [cur, "lo"], ["wl"], T.wl[:], T[cur][:, 0:C].indirect(T.lo[:, 0:1]), F.Copy)
+        yield from part(T.wl[:], ["wl"], 16, [("lo", T.lo[:, 0:1], (T.lc[:, 0:1], A.add))])
+        for lev in range(8):
+            m = 1 << lev
+            if lev < 4:
+                dst, k = (T.wl[:], "wl") if lev < 3 else (T.rw[:, C - 16:C], ("rw", 16))
+                op("s", "act", [cur, cur + "i", "lo"], [k], dst, T[cur][:, 0:2 * C].indirect(T.lo[:, 0:1]), F.Copy)
+                outs = [("lo", T.lo[:, 0:1], (T.lc[:, lev + 1:lev + 2], A.add) if lev < 3 else minus)]
+                if lev == 3:
+                    outs.append(("ro", T.ro[:, 19:20], minus))
+                new = part(dst, [k], 16, outs)
+            if lev >= 4:
+                op("s", "act", [cur, off], [nxt], T[nxt][:, 0:C], T[cur][:, 0:C].indirect(T[off][:]), F.Copy)
+                if lev < 7:
+                    yield from part(T[nxt][:, 0:C], [nxt], C, [("rofs", T.rofs[:], minus)])
+                lst, lk = (T.lo[:, 0:1], "lo") if m == 16 else (T.ro[:, 20 - m // 16:20], "ro")
+                dst, k = T.rw[:, C - 2 * m:C - m], ("rw", 2 * m)
+                op("s", "act", [cur, lk], [k], dst, T[cur][:, 0:C].indirect(lst), F.Copy)
+                new = part(dst, [k], m, [("ro", T.ro[:, 20 - m // 8:20 - m // 16], minus)])
+            if lev < 4:
+                op("s", "act", [cur, off], [nxt], T[nxt][:, 0:C], T[cur][:, 0:C].indirect(T[off][:]), F.Copy)
+            yield from new
+            cur, nxt, off = nxt, cur, "rofs"
+            if lev < 4:
+                yield from part(T[cur][:, 0:C], [cur], C, [("rofs", T.rofs[:], minus)])
+        op("s", "act", [cur, "ro"], [("rw", 320)], T.rw[:, 0:64], T[cur][:, 0:C].indirect(T.ro[:, 16:20]), F.Copy)
+        yield from part(T.rw[:, 0:64], [("rw", 320)], 64, [("ro", T.ro[:, 0:4], minus)])
+        op("v", "set", [], ["km"], T.km[:, 0:1], float(C - 1)); yield
+        op("v", "copy", ["km", "ro"], ["pw"], T.pw[:].indirect(T.ro[:]), T.km[:]); yield
+        op("v", "ts", ["ro"], ["ordo"], T.ordo[:], T.ro[:], -1.0, float(PADZ + C - 1), A.mult, A.add); yield
+        yield from part(T.pw[:], ["pw"], C, [("pmo", T.pmo[:], minus)])
+        op("v", "tt", [("rw", n) for n in (16, 32, 64, 128, 256, 320)] + ["rw2"], ["wd"], T.wd[:], T.rw[:, 0:C], T.rw[:, 1:C + 1], A.subtract); yield
+
+    def alt(z, le, o):
+        op("v", "tt", [z, "eif"], ["xle"], T.xle[:], T[z][:], T.eif[:], A.is_le); yield
+        op("v", "ts", ["xle"], ["xle"], T.xle[:], T.xle[:], 1000.0, None, A.mult); yield
+        op("v", "tt", ["xle", z], ["xle"], T.xle[:], T.xle[:], T[z][:], A.add); yield
+        op("v", "ts", ["xle"], [o], T[o][:], T.xle[:], float(C), None, A.min); yield
+
+    def tables():
+        op("s", "act", ["mtw", "ivo"], ["ivmw"], T.ivmw[:], T.mtw[:].indirect(T.ivo[:]), F.Copy)
+        yield from alt("ivs", "xle", "xao")
+        scan("sc", T.ivmw[:], ["ivmw"]); yield
+        op("v", "ts", ["sc", "bigc"], ["t1"], T.t1[:], T.sc[:, 15::16], T.bigc[:, 0:1], None, A.subtract); yield
+        yield from alt("t1", "xle", "xbo")
+        op("v", "tt", ["t1", "ivs"], ["ivd"], T.ivd[:], T.t1[:], T.ivs[:], A.subtract); yield
+        op("s", "act", ["iotc", "iotc2", "xao"], ["xa"], T.xa[:], T.iotc[:, 0:328].indirect(T.xao[:]), F.Copy)
+        op("s", "act", ["iotc", "iotc2", "xbo"], ["xb"], T.xb[:], T.iotc[:, 0:328].indirect(T.xbo[:]), F.Copy)
+        op("v", "tt", ["xa", "iotj"], ["da"], T.da[:], T.xa[:], T.iotj[:], A.subtract); yield
+        op("v", "tt", ["xb", "xa"], ["dd"], T.dd[:], T.xb[:], T.xa[:], A.subtract); yield
+
+    def udtables():
+        op("v", "copy", ["udin"], ["udo"], T.udo[:], T.udin[:]); yield
+        op("v", "copy", ["udin"], ["uds"], T.uds[:], T.udin[:]); yield
+        op("s", "act", ["iotj", "udo"], ["xa"], T.xa[:], T.iotj[:].indirect(T.udo[:]), F.Copy)
+        op("s", "act", ["xa", "mto"], ["xb"], T.xb[:], T.xa[:].indirect(T.mto[:]), F.Copy)
+        scan("sce", T.xb[:], ["xb"]); yield
+        op("v", "ts", ["sce", "bigc"], ["sn"], T.sn[:], T.sce[:, 15::16], T.bigc[:, 0:1], None, A.subtract); yield
+        op("v", "tt", ["sn", "uds"], ["udd"], T.udd[:], T.sn[:], T.uds[:], A.subtract); yield
+
+    def run(main, *side):
+        side = [s for s in side]
+        for _ in main:
+            while side:
+                try:
+                    next(side[0])
+                    break
+                except StopIteration:
+                    side.pop(0)
+        for s in side:
+            for _ in s:
+                pass
+
+    def quantise_x(k, tile):
+        op("v", "quant", [tile], ["qx%d" % k, "sx%d" % k], T["qx%d" % k][:], T["sx%d" % k][:], T[tile][:])
+
+    def mm(bank, w, ws, x, xs, wv, wsv, xv, xsv, n):
+        op("t", "mm", [w, ws, x, xs], ["ps%d" % bank], T["ps%d" % bank][:, 0:n], wv, wsv, xv, xsv, True, True)
+
+    def unpack(bank, i, qn, sn):
+        mm(bank, "qe%d" % i, "se%d" % i, qn, sn, T.qe[:, 128 * i:128 * i + 128], T.se[:, 128 * i:128 * i + 128], T[qn][:], T[sn][:], C)
+
+    def th_copy(dst, i, bank):
+        op("s", "act", ["ps%d" % bank], [(dst, i)], T[dst][:, C * i:C * i + C], T["ps%d" % bank][:, 0:C], F.Copy, scale=0.5)
+
+    def pick(dst, src, i, off):
+        op("s", "act", [(src, i), off], [(dst, i)], T[dst][:, C * i:C * i + C], T[src][:, C * i:C * i + C].indirect(li(off)), F.Copy)
+
+    OWNB, PARB = [1, 2, 3, 4], [5, 6, 7, 0]
+
+    def keys(s, sets):
+        return [("d%d" % s, k) for k in sets]
+
+    def stage(s):
+        w = C // RAD[s]
+        nb = C // SIZES[s]
+        if w // 16 % 2:
+            op("v", "ts", ["t1"], ["ob"], T.ob[:, 1:21], T.t1[:], -float(nb), None, A.mult); yield
+        op("v", "ts", ["t1"], ["oa"], T.oa[:, 0:20], T.t1[:], -float(nb), None, A.mult); yield
+        for k in range(1, RAD[s]):
+            c0 = k * w // 16
+            o, lo = ("oa", c0) if c0 % 2 == 0 else ("ob", c0 + 1)
+            d = T["d%d" % s]
+            lim = PADZ + k * w
+            op("v", "tt", keys(s, range(-1, k + 1)) + [o], keys(s, [k]), d[:, lim:lim + w], d[:, 0:lim].indirect(T[o][:, lo:lo + w // 16]), d[:, lim:lim + w], A.add); yield
+
+    def turn(s):
+        q = RAD[s + 1]
+        w = C // q
+        src, o, ks = (T.da, 0, ["da"]) if s < 0 else (T["d%d" % s], PADZ, keys(s, range(RAD[s])))
+        for i in range(q):
+            v = src[:, o + q - 1 - i:o + C:q]
+            op("v", "scan", ks + ["msk"], [("sc", i)] + (["sc"] if i == 0 else []), T.sc[:, w * i:w * i + w], T.msk[:, 0:w], v, 0.0, A.add, A.max); yield
+            op("s", "act", ks, keys(s + 1, [i]), T["d%d" % (s + 1)][:, PADZ + w * i:PADZ + w * i + w], v, F.Copy)
+        k = "k%d" % (s + 1)
+        op("v", "tt", [("sc", i) for i in range(q)] + ["sc", k], ["t1"], T.t1[:], T.sc[:, 15::16], T.kk[:, 20 * s + 20:20 * s + 40], A.add); yield
+
+    def edit_iv(r):
+        op("v", "scan", ["giv", "msks"], ["scs"], T.scs[:], T.msks[:], T.giv[:], 0.0, A.add, A.max); yield
+        op("v", "ts", ["scs", "bigs"], ["sf"], T.sf[:], T.scs[:, 15::16], T.bigs[:, 0:1], None, A.subtract); yield
+        op("v", "tt", ["sf", "ivd"], ["sm"], T.sm[:], T.sf[:], T.ivd[:], A.mult); yield
+        op("v", "tt", ["ivs", "sm"], ["ivs"], T.ivs[:], T.ivs[:], T.sm[:], A.add); yield
+        op("v", "copy", ["ivs"], ["ivn%d" % r], li("ivn%d" % r), T.ivs[:])
+        send(rank ^ STEP[r], "ivn%d" % r, li("ivp%d" % r), li("ivn%d" % r), "ai%d" % r); yield
+        if r < 2:
+            op("v", "ts", ["sm"], ["sn"], T.sn[:], T.sm[:], -2.0, None, A.mult); yield
+            op("v", "tt", ["ivd", "sn"], ["ivd"], T.ivd[:], T.ivd[:], T.sn[:], A.add); yield
+
+    def edit_ud(r):
+        op("v", "scan", ["sw", "msks"], ["scs"], T.scs[:], T.msks[:], T.sw[:], 0.0, A.add, A.max); yield
+        op("v", "ts", ["scs", "bigs"], ["sf"], T.sf[:], T.scs[:, 15::16], T.bigs[:, 0:1], None, A.subtract); yield
+        op("v", "tt", ["sf", "udd"], ["sm"], T.sm[:], T.sf[:], T.udd[:], A.mult); yield
+        op("v", "tt", ["uds", "sm"], ["uds"], T.uds[:], T.uds[:], T.sm[:], A.add); yield
+        op("v", "copy", ["uds"], ["udn"], T.udn[:], T.uds[:]); yield
+        if r < 2:
+            op("v", "ts", ["sm"], ["sn"], T.sn[:], T.sm[:], -2.0, None, A.mult); yield
+            op("v", "tt", ["udd", "sn"], ["udd"], T.udd[:], T.udd[:], T.sn[:], A.add); yield
+
+    def signs(r):
+        ivo = "ivo" if r == 0 else "ivn%d" % (r - 1)
+        op("v", "ts", ["ps0"], ["pp"], T.pp[:], T.ps0[:, 0:C], 0.0, None, A.is_le); yield
+        op("s", "act", ["ps5"], ["sg"], T.sg[:], T.ps5[:, 0:C], F.Sign)
+        op("v", "tt", ["pp", "mto", "sg"], ["sw"], T.sw[:], T.pp[:].indirect(T.mto[:]), T.sg[:], A.is_lt); yield
+        op("s", "act", ["sw", ivo], ["giv"], T.giv[:], T.sw[:].indirect(li(ivo)), F.Copy)
+        op("v", "tt", ["sw", ivo, "dd"], ["tt"], T.tt[:], T.sw[:].indirect(li(ivo)), T.dd[:], A.mult); yield
+        op("v", "tt", ["tt", "da"], ["da"], T.da[:], T.da[:], T.tt[:], A.add); yield
+        yield from turn(-1)
+
+    def undos(r):
+        qp, sp = "qp%d" % r, "sp%d" % r
+        th_copy("th", 0, OWNB[0])
+        th_copy("th", 1, OWNB[1])
+        yield from stage(0)
+        yield from turn(0)
+        th_copy("th", 2, OWNB[2])
+        th_copy("th", 3, OWNB[3])
+        yield from stage(1)
+        yield from turn(1)
+        for i in range(4):
+            unpack(PARB[i], i, qp, sp)
+        yield from stage(2)
+        yield from turn(2)
+        for i in range(4):
+            th_copy("thp", i, PARB[i])
+        yield from stage(3)
+        for i in range(4):
+            pick("tiv", "thp", i, "ivp%d" % r)
+
+    def bypass(r):
+        op("v", "ts", keys(3, range(-1, 5)) + ["ordo"], ["vi"], T.vi[:], T.d3[:, 0:PADZ + C].indirect(T.ordo[:]), 1024.0, None, A.mult); yield
+        op("v", "ts", ["vi"], ["vi"], T.vi[:], T.vi[:], 1, None, A.bitwise_and); yield
+        op("v", "scan", ["vi", "wd"], ["st"], T.st[:], T.vi[:], T.wd[:], 0.0, A.mult, A.add); yield
+        op("v", "tt", ["st", "pmo", "iotj"], ["bw"], T.bw[:], T.st[:].indirect(T.pmo[:]), T.iotj[:], A.add); yield
+        scan("sce", T.bw[:], ["bw"]); yield
+        op("v", "ts", ["sce", "bigc"], ["bn%d" % r], li("bn%d" % r), T.sce[:, 15::16], T.bigc[:, 0:1], None, A.subtract)
+        send(rank ^ STEP[r], "bn%d" % r, li("bp%d" % r), li("bn%d" % r), "ab%d" % r); yield
+
+    def partner_e(r):
+        op("s", "act", ["bw", "ivp%d" % r], ["ew"], T.ew[:], T.bw[:].indirect(li("ivp%d" % r)), F.Copy)
+        yield from edit_ud(r)
+        scan("sce", T.ew[:], ["ew"]); yield
+        op("v", "ts", ["sce", "bigc"], ["en%d" % r], li("en%d" % r), T.sce[:, 15::16], T.bigc[:, 0:1], None, A.subtract)
+        send(rank ^ STEP[r], "en%d" % r, li("ep%d" % r), li("en%d" % r), "ae%d" % r); yield
+
+    def flat(*gens):
+        for x in gens:
+            yield from x
+
+    def prepare():
+        quantise_x(0, "xin"); yield
+        op("v", "quant", ["uin"], ["qu", "su"], T.qu[:], T.su[:], T.uin[:])
+        op("v", "copy", ["c16"], ["uof"], T.uof[:], T.c16[:, 0:8])
+        op("v", "copy", ["qu", "uof"], ["qr"], T.qr[:].bitcast(dt.uint32), T.qu[:].bitcast(dt.uint32).indirect(T.uof[:]))
+        op("s", "act", ["su", "uof"], ["sr"], T.sr[:], T.su[:].indirect(T.uof[:]), F.Copy)
+
+    def constants():
+        for i in range(4):
+            op("v", "quant", ["eb"], ["qe%d" % i, "se%d" % i], T.qe[:, 128 * i:128 * i + 128], T.se[:, 128 * i:128 * i + 128], T.eb[:, 3 - i:3 - i + 512]); yield
+
+    def exchange(r):
+        p = rank ^ STEP[r]
+        qx, sx = "qx%d" % r, "sx%d" % r
+        send(p, qx, T["qp%d" % r][:].bitcast(dt.uint8), T[qx][:].bitcast(dt.uint8), "aq%d" % r)
+        send(p, sx, T["sp%d" % r][:], T[sx][:], "as%d" % r); yield
+        for bank in (0, 5):
+            mm(bank, "qr", "sr", qx, sx, T.qr[:], T.sr[:], T[qx][:], T[sx][:], C)
+
+    def own(r):
+        for i in range(4):
+            unpack(OWNB[i], i, "qx%d" % r, "sx%d" % r); yield
+
+    for r in range(3):
+        if r == 0:
+            merge(chain(ring()),
+                  chain(prepare(), exchange(0), ("mark", "x"), constants(), own(0), ("mark", "own")),
+                  chain(places(), tables(), places2(), ("after", "x"), signs(0), ("mark", "giv"), ("after", "own"), undos(0)),
+                  chain(("after", "giv"), edit_iv(0), udtables()))
+        else:
+            merge(chain(exchange(r), own(r), signs(r), ("mark", "giv"), undos(r)), chain(("after", "giv"), edit_iv(r)))
+        for _ in bypass(r):
+            pass
+        for _ in partner_e(r):
+            pass
+        for i in range(4):
+            pick("tu", "th", i, "udn")
+        if r < 2:
+            op("s", "act", ["tt"], ["sg"], T.sg[:], T.tt[:], F.Copy, scale=-2.0)
+        else:
+            op("s", "act", ["iotj", "udn"], ["xa"], T.xa[:], T.iotj[:].indirect(T.udn[:]), F.Copy)
+            dma("y", "duo", ["xa"], [], T.uo[:, :], T.xa[0:128:16, :])
+            op("v", "quant", ["vin"], ["qv_", "sv"], T.qv_[:], T.sv[:], T.vin[:])
+        for h in range(2):
+            for i in range(4):
+                c0 = 160 * h
+                op("v", "tt", [("thp", i), ("tiv", i), "bp%d" % r], [("zt", h, i)], T.zt[:, 4 * c0 + i:4 * c0 + 640:4],
+                   T.thp[:, C * i:C * i + C].indirect(li("bp%d" % r, 10 * h, 10 * h + 10)), T.tiv[:, C * i + c0:C * i + c0 + 160], A.add)
+            op("v", "quant", [("zt", h, i) for i in range(4)], ["qz%d" % h, "sz%d" % h], T.qz[:, 160 * h:160 * h + 160], T.sz[:, 160 * h:160 * h + 160], T.zt[:, 640 * h:640 * h + 640])
+            for i in range(4):
+                bank = (OWNB, PARB)[h][i]
+                mm(bank, "qw", "sw_", "qz%d" % h, "sz%d" % h, T.qw[:, 128 * i:128 * i + 128], T.sw_[:, 128 * i:128 * i + 128], T.qz[:, 160 * h:160 * h + 160], T.sz[:, 160 * h:160 * h + 160], 160)
+                op("s", "act", ["ps%d" % bank], [("hh", i, h)], T.hh[:, C * i + 160 * h:C * i + 160 * h + 160], T["ps%d" % bank][:, 0:160], F.Copy, scale=2.0 ** -6)
+        if r < 2:
+            op("v", "tt", ["dd", "sg"], ["dd"], T.dd[:], T.dd[:], T.sg[:], A.add)
+        for i in range(4):
+            op("v", "tt", [("hh", i, 0), ("hh", i, 1), ("tu", i), "ep%d" % r], [("xt", i)], T.xt[:, i::4],
+               T.hh[:, C * i:C * i + C].indirect(li("ep%d" % r)), T.tu[:, C * i:C * i + C], A.add)
+        n = r + 1
+        op("v", "quant", [("xt", i) for i in range(4)], ["qx%d" % n, "sx%d" % n], T["qx%d" % n][:], T["sx%d" % n][:], T.xt[:])
+
+    dma("y", "doc", ["qx3"], [], T.oc[:], T.qx3[:].bitcast(dt.uint8))
+    for k in range(4):
+        dma("s" if k < 2 else "y", "ds%d" % k, ["sx3"], [], T.osc[4 * k:4 * k + 4, :], T.sx3[32 * k:32 * k + 4, :])
+    mm(0, "qv_", "sv", "qx3", "sx3", T.qv_[:], T.sv[:], T.qx3[:], T.sx3[:], C)
+    op("v", "copy", ["ps0"], ["ys"], T.ys[:], T.ps0[:, 0:C])
+    dma("y", "dy0", ["ys"], [], T.y[:], T.ys[:])
+    for s, n in total.items():
+        g.wait_ge(T.sem[s], n)

@@ -1,15 +1,16 @@
-from concourse.bass import DstId, RemoteDMATransfer
 from concourse.mybir import dt, AluOpType as A, ActivationFunctionType as F
 
 C = 320
+H = C // 2
 RAD = [4, 4, 4, 5]
 SIZES = [4, 16, 64, 320]
 STEP = [1, 2, 4]
 PADZ = 16
-BIG, LOW = 1024.0, -8192.0
-BIGS, LOWS = 4.0, -64.0
-FRAC = 1.0 / 1024.0
+K = 1024.0
+BIG, LOW = 2.0 ** 20, -2.0 ** 22
+BIGS = 4.0
 F4, U8, BF, F32, I32, U16 = "float8_e4m3fn_x4", "uint8", "bfloat16", "float32", "int32", "uint16"
+DI, OF, IV, UD, ALL = (0, 24), (24, 48), (48, 68), (68, 88), (0, 88)
 
 SCRATCH = {}
 SEMAPHORES = ["qv", "qs", "qt", "qg", "sent"]
@@ -23,36 +24,92 @@ for _n in ("ud", "iv", "hp", "mt"):
     _buf(_n + "in", 20, I32)
     _buf(_n + "o", 20, U16)
     SEMAPHORES.append("d" + _n)
-for _n in ("x", "u", "v", "wc", "ws", "y0", "y1", "oc", "s0", "s1", "s2", "s3", "uo"):
+for _n in ("x", "u", "v", "wc", "ws", "y0", "y1", "oc0", "oc1", "s0", "s1", "s2", "s3", "uo"):
     SEMAPHORES.append("d" + _n)
 for _n, _w, _t in (("xin", 1280, BF), ("uin", 512, BF), ("vin", 512, BF), ("eb", 520, BF), ("ones", 520, BF),
-                   ("iotj", C, F32), ("iotc", 328, F32), ("ti", 16, I32), ("c16", 20, I32), ("pa", 20, I32), ("po", 20, U16), ("m16", 32, F32),
-                   ("msk", C, F32), ("msks", C, BF),
-                   ("pf", 2, F32), ("bigc", 2, F32), ("bigs", 2, F32), ("eif", 20, F32), ("kk", 80, F32),
-                   ("mtw", C, F32), ("ivmw", C, F32), ("xa", C, F32), ("xb", C, F32),
-                   ("fa", 2 * C, F32), ("fb", 2 * C, F32), ("sg", C, F32), ("rsc", C, F32), ("rofs", 20, U16), ("wl", 16, F32), ("lo", 2, U16),
-                   ("lci", 4, I32), ("lc", 4, F32), ("ro", 20, U16), ("pw", C, F32), ("km", C, F32), ("pmo", 20, U16), ("rw", 328, F32), ("wd", C, F32), ("ordo", 20, U16),
-                   ("da", C, F32), ("dd", C, F32), ("tt", C, F32), ("sc", C, F32), ("scs", C, BF), ("t1", 20, F32),
-                   ("ivs", 20, F32), ("ivd", 20, F32), ("uds", 20, F32), ("udd", 20, F32), ("sf", 20, F32), ("sm", 20, F32), ("sn", 20, F32),
-                   ("xle", 20, F32), ("xao", 20, U16), ("xbo", 20, U16), ("oa", 22, U16), ("ob", 22, U16),
-                   ("pp", C, BF), ("sw", C, BF), ("giv", C, BF), ("vi", C, I32), ("st", C, F32), ("bw", C, F32), ("ew", C, F32), ("sce", C, F32),
+                   ("pw", 10 * C, F32), ("iden", C, F32), ("tab", C, F32), ("ti", 16, I32), ("pa", 20, I32), ("po", 20, U16), ("m16", 32, F32),
+                   ("msk", C, F32), ("msks", C, BF), ("col", 8, F32), ("ci", 4, I32), ("c8", 8, I32), ("uof", 8, U16),
+                   ("jj", 48, F32), ("pp", 48, F32), ("kk", 56, F32), ("d48", 48, F32), ("z48", 48, F32), ("w48", 48, F32), ("t20", 20, F32),
+                   ("mtw", C, F32), ("aw", C, F32), ("bw0", C, F32), ("uw", C, F32), ("umw", C, F32), ("sab", 768, F32),
+                   ("ro4", 20, U16), ("ro16", 20, U16), ("x0", 2, U16), ("x1", 2, U16), ("lo", 2, U16), ("wl", 16, F32), ("rsc", C, F32),
+                   ("ro", 20, U16), ("rw", 328, F32), ("km", C, F32), ("pm", C, F32), ("pmo", 20, U16), ("wd", C, F32), ("ordo", 20, U16),
+                   ("mid", 88, F32), ("dif", 88, F32), ("cen", 88, F32), ("mul", 88, F32), ("val", 88, F32),
+                   ("sg", C, BF), ("np_", C, BF), ("sw", C, BF), ("sa", C, BF), ("scs", 384, BF), ("scn", 2 * C, BF), ("e0", C, F32),
+                   ("sc", 288, F32), ("t1", 18, F32), ("oa", 18, U16), ("ne", C, I32), ("st", C, F32), ("bw", C, F32), ("ew", C, F32),
+                   ("sb", C, F32), ("se_", C, F32),
                    ("th", 1280, BF), ("thp", 1280, BF), ("tiv", 1280, BF), ("tu", 1280, BF), ("hh", 1280, BF), ("xt", 1280, BF), ("zt", 1280, BF),
-                   ("uof", 8, U16), ("ys", C, F32),
+                   ("ys", C, F32),
                    ("qu", 128, F4), ("su", 128, U8), ("qr", 128, F4), ("sr", 128, U8), ("qv_", 128, F4), ("sv", 128, U8),
-                   ("qw", 512, F4), ("sw_", 512, U8), ("qe", 512, F4), ("se", 512, U8), ("qz", C, F4), ("sz", C, U8), ("udn", 20, U16)):
+                   ("qw", 512, F4), ("sw_", 512, U8), ("qe", 512, F4), ("se", 512, U8), ("qz", C, F4), ("sz", C, U8)):
     _buf(_n, _w, _t)
-for _n in ("ivn", "ivp", "bn", "bp", "en", "ep"):
-    _buf(_n, 72, U16)
 for _i in range(4):
-    _buf("d%d" % _i, 16 + C, F32)
+    _buf("d%d" % _i, PADZ + C, I32 if _i == 3 else F32)
     _buf("qx%d" % _i, C, F4)
     _buf("sx%d" % _i, C, U8)
 for _i in range(3):
     _buf("qp%d" % _i, C, F4)
     _buf("sp%d" % _i, C, U8)
-    SEMAPHORES += ["%s%d" % (_n, _i) for _n in ("aq", "as", "ai", "ab", "ae")]
+    _buf("lst%d" % _i, 128, U16)
+    _buf("land%d" % _i, 72, U16)
+    SEMAPHORES += ["%s%d" % (_n, _i) for _n in ("aq", "as", "ai", "ab", "ac", "ae")]
 for _i in range(8):
     SCRATCH["ps%d" % _i] = ("psum", [128, 512], F32)
+
+WAKE = 0.06
+CFG = {"split": 0, "wait": 0.5, "passes": 3}
+
+
+def lasts(name, n, kind):
+    if kind == "gather":
+        return 0.06 + 0.0016 * n
+    if kind == "scatter":
+        return 0.06 + 0.004 * n
+    if name == "quant":
+        return 0.015 + 0.0011 * n
+    if name == "mm":
+        return 0.0006 * (n + 16)
+    if name in ("iota", "sel"):
+        return 0.16 + 0.0021 * n
+    return max(0.067, n * (0.0021 if name == "tt" else 0.00052 if kind == "short" else 0.00104))
+
+
+def order(calls):
+    n = len(calls)
+    after = [[] for c in calls]
+    for i, c in enumerate(calls):
+        for d in c["deps"]:
+            after[d].append(i)
+
+    def place(urge, back):
+        before, behind = (after, [c["deps"] for c in calls]) if back else ([c["deps"] for c in calls], after)
+        left, free, begin = [len(b) for b in before], {}, {}
+        ready = {i: calls[i]["lat"] * back for i in range(n) if not left[i]}
+        while ready:
+            est = {i: max(t, free.get(calls[i]["q"], 0.0)) for i, t in ready.items()}
+            j = min(est, key=lambda i: (est[i] + calls[i]["dur"], i))
+            near = [i for i in est if calls[i]["q"] == calls[j]["q"]]
+            first = min(est[i] for i in near)
+            i = max((i for i in near if est[i] <= first + CFG["wait"] * (est[j] + calls[j]["dur"] - first)), key=lambda i: (urge[i], -i))
+            begin[i], free[calls[i]["q"]] = est[i], est[i] + calls[i]["dur"]
+            del ready[i]
+            for d in behind[i]:
+                left[d] -= 1
+                if not left[d]:
+                    ready[d] = calls[d]["lat"] * back + max(begin[k] + calls[k]["dur"] + calls[k]["lat"] * (not back) + WAKE for k in before[d])
+        return [begin[i] + calls[i]["dur"] for i in range(n)], begin
+
+    urge = [0.0] * n
+    for i in reversed(range(n)):
+        urge[i] = calls[i]["dur"] + calls[i]["lat"] + max([0.0] + [urge[d] + WAKE for d in after[i]])
+    best = None
+    for _ in range(CFG["passes"]):
+        ends, begin = place(urge, False)
+        end = max(ends[i] + calls[i]["lat"] for i in range(n))
+        if best is None or end < best[0]:
+            best = (end, begin)
+        urge = place(ends, True)[0]
+    CFG["est"] = best[0]
+    return sorted(range(n), key=lambda i: (best[1][i] if calls[i]["deps"] or not calls[i]["lat"] else 0.0, i))
 
 
 def rank_program(g, core, T, topo):
@@ -61,459 +118,350 @@ def rank_program(g, core, T, topo):
         return
     V, S, P, Y = g.vector, g.scalar, g.tensor, g.sync
     eng = {"v": V, "s": S, "t": P, "g": g, "y": Y}
-    count = {"qv": 0, "qs": 0, "qt": 0, "qg": 0}
-    seen = {q: {} for q in eng}
-    lastw, readers = {}, {}
-    total = {}
+    fns = {"copy": V.tensor_copy, "tt": V.tensor_tensor, "ts": V.tensor_scalar, "scan": V.tensor_tensor_scan, "set": V.memset,
+           "quant": V.quantize_mx, "act": S.activation, "mm": P.matmul_mx, "iota": g.iota, "sel": g.affine_select}
+    calls, lastw, readers = [], {}, {}
 
-    def need(q, rd, wr):
-        dep = {}
-        for k in rd:
-            for s, n in lastw.get(k, ()):
-                dep[s] = max(dep.get(s, 0), n)
+    def note(q, rd, wr, dur, lat, issue):
+        deps = {lastw[k] for k in rd}
         for k in wr:
-            for s, n in list(lastw.get(k, ())) + readers.get(k, []):
-                dep[s] = max(dep.get(s, 0), n)
-        for s, n in dep.items():
-            if seen[q].get(s, 0) < n:
-                eng[q].wait_ge(T.sem[s], n)
-                seen[q][s] = n
-
-    def note(tok, rd, wr):
+            deps.update(readers.get(k, []) + ([lastw[k]] if k in lastw else []))
         for k in rd:
-            readers.setdefault(k, []).append(tok)
+            readers.setdefault(k, []).append(len(calls))
         for k in wr:
-            lastw[k] = [tok]
-            readers[k] = []
+            lastw[k], readers[k] = len(calls), []
+        calls.append({"q": q, "deps": deps, "dur": dur, "lat": lat, "issue": issue})
 
-    rec, free, fin = [None], {q: 0.0 for q in eng}, {}
-    usual = {"copy": 0.1, "tt": 0.65, "ts": 0.1, "scan": 0.35, "set": 0.08, "quant": 0.2, "act": 0.6, "mm": 0.35, "iota": 0.8, "sel": 1.2}
-    small = ("t1", "sf", "sm", "sn", "ivs", "ivd", "uds", "udd", "xle")
-    quarter = [("sc", i) for i in range(5)] + [("d%d" % s, i) for s in range(4) for i in range(5)]
+    count = {}
 
-    def start(q, rd, wr):
-        t = free[q]
-        for k in rd:
-            for x in lastw.get(k, ()):
-                t = max(t, fin.get(x, 0.0) + 0.06)
-        for k in wr:
-            for x in list(lastw.get(k, ())) + readers.get(k, []):
-                t = max(t, fin.get(x, 0.0) + 0.06)
-        return t
+    def op(name, n, rd, wr, *a, kind="", **kw):
+        q = {"act": "s", "mm": "t", "iota": "g", "sel": "g"}.get(name, "v")
 
-    def lasts(name, wr):
-        if name == "tt" and wr[0] in small:
-            return 0.1
-        if wr and (wr[0] in quarter or wr[0] == "wl"):
-            return 0.2 if name == "tt" else 0.12
-        return usual[name]
+        def issue():
+            count["q" + q] = count.get("q" + q, 0) + 1
+            fns[name](*a, **kw).then_inc(T.sem["q" + q], 1)
+            return "q" + q, count["q" + q]
+        note(q, rd, wr, lasts(name, n, kind), 0.0, issue)
 
-    def merge(*chains):
-        chains, done = [list(c) for c in chains], set()
-        while any(chains):
-            best = None
-            for c in chains:
-                while c and c[0][0] == "mark":
-                    done.add(c.pop(0)[1])
-                if c and c[0][0] == "after":
-                    if c[0][1] not in done:
-                        continue
-                    c.pop(0)
-                if c:
-                    f, a = c[0]
-                    t = start(a[0], a[2], a[3]) if f is op else (start(a[0], a[2], []) if f is dma else 0.0)
-                    if best is None or t < best[0] - 1e-6:
-                        best = (t, c)
-            if best is None:
-                continue
-            f, a = best[1].pop(0)
-            f(*a[:-1], **a[-1])
+    def dma(q, sem, rd, wr, out, in_, lat=2.0):
+        def issue():
+            count[sem] = 16
+            eng[q].dma_start(out, in_).then_inc(T.sem[sem], 16)
+            return sem, 16
+        note(q, rd, wr, 0.05, lat, issue)
 
-    def chain(*parts):
-        out = []
-        for p in parts:
-            if isinstance(p, tuple):
-                out.append(p)
-                continue
-            rec[0] = out
-            for _ in p:
-                pass
-            rec[0] = None
-        return out
+    def send(r, key, land, out, in_, sem, lat=2.1):
+        dst = T.cores[rank ^ STEP[r]]
 
-    def op(q, name, rd, wr, *a, **kw):
-        if rec[0] is not None:
-            rec[0].append((op, (q, name, rd, wr) + a + (kw,)))
-            return
-        t = start(q, rd, wr)
-        free[q] = t + lasts(name, wr)
-        fin[("q" + q, count["q" + q] + 1)] = free[q]
-        need(q, rd, wr)
-        f = {"copy": V.tensor_copy, "tt": V.tensor_tensor, "ts": V.tensor_scalar, "scan": V.tensor_tensor_scan, "set": V.memset,
-             "quant": V.quantize_mx, "act": S.activation, "mm": P.matmul_mx, "iota": g.iota, "sel": g.affine_select}[name]
-        s = "q" + q
-        count[s] += 1
-        f(*a, **kw).then_inc(T.sem[s], 1)
-        total[s] = count[s]
-        note((s, count[s]), rd, wr)
+        def issue():
+            rid, pid = topo.addr(dst)[:2]
+            count["sent"] = count.get("sent", 0) + len(topo.engines(core, dst))
+            count[sem] = len(topo.engines(dst, core))
+            g.remote_dma(out, in_, T.sem[sem], T.sem.sent, pid, rid, topo.mask(core, dst))
+            return sem, count[sem]
+        note("g", key, [land], 0.1, lat, issue)
 
-    def dma(q, sem, rd, wr, out, in_):
-        need(q, rd, wr)
-        total[sem] = total.get(sem, 0) + 16
-        free[q] += 0.06
-        fin[(sem, total[sem])] = free[q] + (3.5 if sem == "dx" else 2.2)
-        eng[q].dma_start(out, in_).then_inc(T.sem[sem], 16)
-        note((sem, total[sem]), rd, wr)
+    def pick(q, n, rd, wr, out, win, off, **kw):
+        if q == "s":
+            op("act", n, rd, wr, out, win.indirect(off), F.Copy, kind="gather", **kw)
+        else:
+            op("copy", n, rd, wr, out, win.indirect(off), kind="gather")
 
-    def send(p, key, out, in_, sem):
-        if rec[0] is not None:
-            rec[0].append((send, (p, key, out, in_, sem, {})))
-            return
-        need("g", [key], [])
-        dst = T.cores[p]
-        rid, pid = topo.addr(dst)[:2]
-        e = topo.engines(core, dst)[:8]
-        total["sent"] = total.get("sent", 0) + len(e)
-        g.remote_dma(out, in_, T.sem[sem], T.sem.sent, pid, rid, sum(1 << i for i in e))
+    def scan(n, rd, wr, out, src):
+        op("scan", n, rd + ["msk"], wr, out, T.msk[:, 0:n], src, 0.0, A.add, A.max)
 
-    def lands(key, sem, p):
-        n = len(topo.engines(T.cores[p], core)[:8])
-        lastw[key] = [(sem, n)]
-        fin[(sem, n)] = 14.0
-        total[sem] = n
+    def scans(n, rd, wr, out, src):
+        op("scan", n, rd + ["msks"], wr, out, T.msks[:, 0:n], src, 0.0, A.add, A.max, kind="short")
 
-    for r in range(3):
-        p = rank ^ STEP[r]
-        for k, s in (("qp", "aq"), ("sp", "as"), ("ivp", "ai"), ("bp", "ab"), ("ep", "ae")):
-            lands("%s%d" % (k, r), "%s%d" % (s, r), p)
+    def offsets(n, rd, wr, out, buf, src, add=None):
+        scan(n, rd, [buf], T[buf][:, 0:n], src)
+        if add is None:
+            op("ts", 1, [buf, "big"], wr, out, T[buf][:, 15:n:16], big, None, A.subtract)
+        else:
+            op("ts", 1, [buf, add[0]], wr, out, T[buf][:, 15:n:16], add[1], None, A.add)
 
-    def li(name, lo=0, hi=20):
-        if name[:-1] in ("ivn", "ivp", "bn", "bp", "en", "ep"):
-            o = 24 * int(name[-1])
-            return T[name[:-1]][:, o + lo:o + hi]
-        return T[name][:, lo:hi]
+    def quant(n, rd, wr, q, s, t):
+        op("quant", n, rd, wr, q, s, t)
+
+    def mm(bank, n, rd, w, ws, x, xs):
+        op("mm", n, rd, ["ps%d" % bank], T["ps%d" % bank][:, 0:n], w, ws, x, xs, True, True)
+
+    def part(buf, p):
+        return T[buf][:, p[0]:p[1]]
+
+    def li(name, c=0, n=20):
+        buf, o = {"bn": ("lst", 88), "en": ("lst", 108), "ivp": ("land", 0), "bp": ("land", 24), "ep": ("land", 48)}[name[:-1]]
+        return T[buf + name[-1]][:, o + c:o + c + n]
+
+    big, bigs, pf, slot = T.col[:, 0:1], T.col[:, 1:2], T.col[:, 2:3], T.col[:, 3:4]
+    iden = T.iden[:]
 
     dma("y", "dhp", [], ["hpin"], T.hpin[:], T.hp[:])
-    dma("s", "div", [], ["ivin"], T.ivin[:], T.iv[:])
-    dma("y", "dx", [], ["xin"], T.xin[:], T.x[:])
     dma("s", "dmt", [], ["mtin"], T.mtin[:], T.mt[:])
-    dma("y", "du", [], ["uin"], T.uin[:], T.u[:])
-    dma("s", "dud", [], ["udin"], T.udin[:], T.ud[:])
-    dma("y", "dws", [], ["sw_"], T.sw_[:], T.ws[:])
-    dma("y", "dwc", [], ["qw"], T.qw[:].bitcast(dt.uint8), T.wc[:])
-    dma("y", "dv", [], ["vin"], T.vin[:], T.v[:])
+    dma("s", "div", [], ["ivin"], T.ivin[:], T.iv[:])
+    dma("y", "dx", [], ["xin"], T.xin[:], T.x[:], 4.0)
+    dma("y", "du", [], ["uin"], T.uin[:], T.u[:], 4.5)
+    dma("s", "dud", [], ["udin"], T.udin[:], T.ud[:], 4.5)
+    dma("y", "dws", ["uin"], ["sw_"], T.sw_[:], T.ws[:])
+    dma("y", "dwc", ["uin"], ["qw"], T.qw[:].bitcast(dt.uint8), T.wc[:], 4.0)
+    dma("y", "dv", ["uin"], ["vin"], T.vin[:], T.v[:], 5.0)
 
-    op("g", "iota", [], ["iotj"], T.iotj[:], [[1, C]], 0, 0, allow_small_or_imprecise_dtypes=True)
-    op("g", "iota", [], ["ti"], T.ti[:], [[1, 16]], 128, -1)
-    op("g", "iota", [], ["pa"], T.pa[:], [[0, 20]], 0, 1)
-    op("g", "iota", [], ["c16"], T.c16[:], [[16, 20]], 0, 0)
-    op("v", "set", [], ["ones"], T.ones[:], 1.0)
-    op("g", "sel", ["ones"], ["eb"], T.eb[:], T.ones[:], [[1, 520]], A.is_equal, 0.0, -3, -4)
-    op("g", "iota", [], ["km"], T.km[:], [[1, C]], -1, 0, allow_small_or_imprecise_dtypes=True)
-    op("v", "set", [], ["iotc2"], T.iotc[:, C:C + 8], float(C))
-    op("v", "set", [], ["rw2"], T.rw[:, C:C + 8], float(C - 1))
-    op("s", "act", ["iotj"], ["iotc"], T.iotc[:, 0:C], T.iotj[:], F.Copy, bias=FRAC)
-    for n in ("hp", "iv", "mt"):
-        op("v", "copy", [n + "in"], [n + "o"], T[n + "o"][:], T[n + "in"][:])
-    op("s", "act", ["iotj", "hpo"], ["fa"], T.fa[:, 0:C], T.iotj[:].indirect(T.hpo[:]), F.Copy)
-    op("s", "act", ["iotj", "mto"], ["mtw"], T.mtw[:], T.iotj[:].indirect(T.mto[:]), F.Copy)
-    op("v", "ts", ["ti"], ["ti"], T.ti[:], T.ti[:], 15, None, A.bitwise_and)
-    op("v", "ts", ["pa"], ["pa"], T.pa[:], T.pa[:], 15, None, A.bitwise_and)
-    op("v", "copy", ["pa"], ["po"], T.po[:], T.pa[:])
-    op("v", "ts", ["ti"], ["sce"], T.sce[:, 0:16], T.ti[:], 0.0, LOW, A.is_equal, A.mult)
-    op("v", "ts", ["ti"], ["ew"], T.ew[:, 0:16], T.ti[:], 1.0, BIG, A.is_equal, A.mult)
-    op("v", "tt", ["sce", "ew"], ["m16"], T.m16[:, 0:16], T.sce[:, 0:16], T.ew[:, 0:16], A.add)
-    op("s", "act", ["m16", "po"], ["msk"], T.msk[:], T.m16[:, 0:16].indirect(T.po[:]), F.Copy)
-    op("v", "ts", ["m16"], ["m16s"], T.m16[:, 16:32], T.m16[:, 0:16], BIGS / BIG, LOWS, A.mult, A.max)
-    op("s", "act", ["m16s", "po"], ["msks"], T.msks[:], T.m16[:, 16:32].indirect(T.po[:]), F.Copy)
-    op("v", "copy", ["pa"], ["pf"], T.pf[:], T.pa[:, 0:2])
-    op("v", "ts", ["pa"], ["bigc"], T.bigc[:], T.pa[:, 0:2], 15.0, BIG, A.is_lt, A.mult)
+    fl = {"allow_small_or_imprecise_dtypes": True}
+    op("iota", 16, [], ["ti"], T.ti[:], [[1, 16]], 128, -1)
+    op("iota", 20, [], ["pa"], T.pa[:], [[0, 20]], 0, 1)
+    op("iota", C, [], ["iden"], iden, [[1, C]], 0, 0, **fl)
+    op("ts", 1, ["ti"], ["ti"], T.ti[:], T.ti[:], 15, None, A.bitwise_and)
+    op("ts", 1, ["pa"], ["pa"], T.pa[:], T.pa[:], 15, None, A.bitwise_and)
+    op("copy", 1, ["pa"], ["po"], T.po[:], T.pa[:])
+    op("ts", 1, ["ti"], ["d48"], T.d48[:, 0:16], T.ti[:], 0.0, LOW, A.is_equal, A.mult)
+    op("ts", 1, ["ti"], ["z48"], T.z48[:, 0:16], T.ti[:], 1.0, BIG, A.is_equal, A.mult)
+    op("tt", 1, ["d48", "z48"], ["m16"], T.m16[:, 0:16], T.d48[:, 0:16], T.z48[:, 0:16], A.add)
+    pick("s", C, ["m16", "po"], ["msk"], T.msk[:], T.m16[:, 0:16], T.po[:])
+    op("ts", 1, ["m16"], ["m16s"], T.m16[:, 16:32], T.m16[:, 0:16], BIGS / BIG, None, A.mult)
+    pick("s", C, ["m16s", "po"], ["msks"], T.msks[:], T.m16[:, 16:32], T.po[:])
+    op("ts", 1, ["pa"], ["big"], big, T.pa[:, 0:1], 15.0, BIG, A.is_lt, A.mult)
+    op("ts", 1, ["pa"], ["bigs"], bigs, T.pa[:, 0:1], 15.0, -BIGS, A.is_lt, A.mult)
+    op("copy", 1, ["pa"], ["pf"], pf, T.pa[:, 0:1])
+    for n in ("hp", "iv", "mt", "ud"):
+        op("copy", 1, [n + "in"], [n + "o"], T[n + "o"][:], T[n + "in"][:])
+    op("set", 260, [], ["ones"], T.ones[:], 1.0)
+    op("sel", 520, ["ones"], ["eb"], T.eb[:], T.ones[:], [[1, 520]], A.is_equal, 0.0, -3, -4)
+    for i in range(4):
+        quant(128, ["eb"], [("qe", i)], T.qe[:, 128 * i:128 * i + 128], T.se[:, 128 * i:128 * i + 128], T.eb[:, 3 - i:3 - i + 512])
+        op("set", 1, [], [("d%d" % i, -1)], T["d%d" % i][:, 0:PADZ], 0)
+    op("set", 192, [], ["scs"] + [("scs", k) for k in range(4)], T.scs[:], 0.0)
+    op("set", 288, [], [("sc", k) for k in range(1, 5)], T.sc[:], 0.0)
+    op("iota", C, [], ["tab"], T.tab[:], [[int(K), C]], 1, 0, **fl)
+    op("set", 1, [], ["tab"], T.tab[:, 0:1], K * C)
+    op("iota", C, [], ["km"], T.km[:], [[1, C]], -1, 0, **fl)
+    op("set", 1, [], ["km"], T.km[:, 0:1], float(C - 1))
+    op("set", 1, [], ["rwend"], T.rw[:, C:C + 8], float(C - 1))
 
-    def places():
-        op("v", "ts", ["c16", "pf"], ["eif"], T.eif[:], T.c16[:], T.pf[:, 0:1], None, A.add); yield
-        op("v", "copy", ["ivin"], ["ivs"], T.ivs[:], T.ivin[:]); yield
+    powers = [1, 2, 3, 4, 8, 12, 0, 16, 32, 48]
 
-    def places2():
-        for i in range(4):
-            op("v", "set", [], [("d%d" % i, -1)], T["d%d" % i][:, 0:PADZ], 0.0); yield
-        op("v", "ts", ["pa"], ["bigs"], T.bigs[:], T.pa[:, 0:2], 15.0, BIGS, A.is_lt, A.mult); yield
-        for i in range(4):
-            nb = C // SIZES[i]
-            op("v", "ts", ["eif"], ["k%d" % i], T.kk[:, 20 * i:20 * i + 20], T.eif[:], -1.0 / nb, -(PADZ + 0.25) / nb, A.mult, A.add); yield
-        op("v", "ts", ["k0", "k1", "k2", "k3", "bigc"], ["k0", "k1", "k2", "k3"], T.kk[:], T.kk[:], T.bigc[:, 0:1], None, A.subtract); yield
+    def power(e):
+        s = powers.index(e % 64 if e != 64 else 1)
+        return T.pw[:, C * s:C * s + C]
 
-    def scan(dst, src, rd, lo=0):
-        op("v", "scan", rd + ["msk"], [dst], T[dst][:], T.msk[:], src, 0.0, A.add, A.max)
+    def raise_to(e, src, off, turn):
+        dst, win = power(e), (iden if src == 0 else power(src))
+        s = powers.index(e if e != 64 else 1) * C
+        rd, wr = [("pw", src, 0), ("pw", src, 1), off], [("pw", e if e != 64 else 1, h) for h in range(2)]
+        if src == 0:
+            rd = ["iden", off]
+        if turn < CFG["split"]:
+            for h, q in enumerate("vs"):
+                pick(q, H, rd, [wr[h]], T.pw[:, s + H * h:s + H * h + H], win, T[off][:, 10 * h:10 * h + 10])
+        else:
+            pick("s", C, rd, wr, dst, win, T[off][:])
 
-    def ring():
-        for n in ("fa", "fb"):
-            op("s", "act", ["iotj"], [n + "i"], T[n][:, C:2 * C], T.iotj[:], F.Copy)
-        op("v", "set", [], ["lo"], T.lo[:], float(C - 1)); yield
+    def pk(*es):
+        return [("pw", e if e != 64 else 1, h) for e in es for h in range(2)]
+
+    op("iota", C, [], pk(0), power(0), [[1, C]], 0, 0, **fl)
+    for turn, (e, src, off) in enumerate(((1, 0, "hpo"), (2, 1, "hpo"), (3, 2, "hpo"), (4, 3, "hpo"), (8, 4, "ro4"), (12, 8, "ro4"), (16, 12, "ro4"),
+                                          (32, 16, "ro16"), (48, 32, "ro16"), (64, 48, "ro16"))):
+        if e == 64:
+            continue
+        raise_to(e, src, off, turn)
+        if e in (4, 16):
+            offsets(C, pk(e), ["ro%d" % e], T["ro%d" % e][:], "rsc", power(e))
+    op("ts", 1, ["pa"], ["ci0"], T.ci[:, 0:1], T.pa[:, 0:1], 3, None, A.bitwise_and)
+    op("ts", 1, ["ci0"], ["x0"], T.x0[:, 0:1], T.ci[:, 0:1], -float(C), 4.0 * C - 1, A.mult, A.add)
+    op("iota", 1, [], ["ci1"], T.ci[:, 2:3], [[0, 1]], 128 + 11, -1)
+    op("ts", 1, ["ci1"], ["ci1"], T.ci[:, 2:3], T.ci[:, 2:3], 2, 3, A.logical_shift_right, A.bitwise_and)
+    op("ts", 1, ["ci1", "big"], ["slot"], slot, T.ci[:, 2:3], float(C), big, A.mult, A.subtract)
+    pick("s", 16, pk(1, 2, 3, 4) + ["x0"], ["wl"], T.wl[:], T.pw[:, 0:4 * C], T.x0[:, 0:1])
+    offsets(16, ["wl"], ["x1"], T.x1[:, 0:1], "sb", T.wl[:], ("slot", slot))
+    pick("s", 16, pk(4, 8, 12, 0) + ["x1"], [("rw", 19)], T.rw[:, C - 16:C], T.pw[:, 3 * C:7 * C], T.x1[:, 0:1])
+    offsets(16, [("rw", 19)], ["lo"], T.lo[:, 0:1], "sb", T.rw[:, C - 16:C])
+    for e in (16, 32, 48):
+        pick("s", 16, pk(e) + ["lo"], [("rw", 19 - e // 16)], T.rw[:, C - 16 - e:C - e], power(e), T.lo[:, 0:1])
+    raise_to(64, 48, "ro16", 9)
+    offsets(64, [("rw", c) for c in range(16, 20)], [("ro", 4)], T.ro[:, 16:20], "sb", T.rw[:, C - 64:C])
+    for k in (3, 2, 1, 0):
+        pick("s", 64, pk(64) + [("ro", k + 1)], [("rw", k)], T.rw[:, 64 * k:64 * k + 64], power(64), T.ro[:, 4 * k + 4:4 * k + 8])
+        offsets(64, [("rw", k)], [("ro", k)], T.ro[:, 4 * k:4 * k + 4], "sb", T.rw[:, 64 * k:64 * k + 64])
+    ro, rw = [("ro", k) for k in range(5)], [("rw", k) for k in (0, 1, 2, 3, 16, 17, 18, 19)]
+    op("ts", 1, ro, ["ordo"], T.ordo[:], T.ro[:], -1.0, float(PADZ + C - 1), A.mult, A.add)
+    op("tt", C, rw + ["rwend"], ["wd"], T.wd[:], T.rw[:, 0:C], T.rw[:, 1:C + 1], A.subtract)
+    op("copy", C, ro + ["km"], ["pm"], T.pm[:].indirect(T.ro[:]), T.km[:], kind="scatter")
+    offsets(C, ["pm"], ["pmo"], T.pmo[:], "rsc", T.pm[:])
+
+    pick("s", C, ["iden", "mto"], ["mtw"], T.mtw[:], iden, T.mto[:])
+    pick("s", C, ["iden", "ivo"], ["aw"], T.aw[:], iden, T.ivo[:])
+    pick("s", C, ["mtw", "ivo"], ["bw0"], T.bw0[:], T.mtw[:], T.ivo[:])
+    op("set", 768, [], ["sab"], T.sab[:], 0.0)
+    for n, w in enumerate(("aw", "bw0")):
         for k in range(4):
-            op("v", "ts", ["pa"], [("lci", k)], T.lci[:, k:k + 1], T.pa[:, 0:1], k, 1, A.logical_shift_right, A.bitwise_and); yield
-        op("v", "ts", [("lci", k) for k in range(4)] + ["bigc"], ["lc"], T.lc[:], T.lci[:], float(C), T.bigc[:, 0:1], A.mult, A.subtract); yield
-        cur, nxt, off = "fa", "fb", "hpo"
+            scan(80, [w, "sab"], [("sab", n, k)], T.sab[:, 384 * n + 96 * k:384 * n + 96 * k + 80], T[w][:, 3 - k::4])
+    op("iota", 48, [], ["jj"], T.jj[:], [[0, 2], [-1, 4], [64, 6]], 3, 0, **fl)
+    op("iota", 48, [], ["pp"], T.pp[:], [[0, 2], [80, 4], [16, 6]], PADZ, 0, **fl)
+    op("ts", 1, ["pf", "big"], ["jb"], T.col[:, 4:5], pf, 4.0, big, A.mult, A.add)
+    op("ts", 1, ["jj", "jb"], ["jj"], T.jj[:], T.jj[:], T.col[:, 4:5], None, A.add)
+    op("ts", 1, ["pp", "pf"], ["pp"], T.pp[:], T.pp[:], pf, None, A.add)
+    op("tt", 1, [("sab", n, k) for n in range(2) for k in range(4)] + ["jj"], ["d48"], T.d48[:], T.sab[:, 15::16], T.jj[:], A.subtract)
+    op("ts", 1, ["d48"], ["z48"], T.z48[:], T.d48[:], -4.0, 4.0, A.mult, A.add)
+    op("ts", 1, ["d48"], ["w48"], T.w48[:], T.d48[:], 0.0, None, A.max)
+    op("tt", 1, ["d48", "z48"], ["z48"], T.z48[:], T.z48[:], T.d48[:], A.max)
+    op("ts", 1, ["z48"], ["z48"], T.z48[:], T.z48[:], -80.0, None, A.mult)
+    op("tt", 1, ["z48", "pp"], ["z48"], T.z48[:], T.z48[:], T.pp[:], A.add)
 
-        def part(src, keys_, n, outs):
-            op("v", "scan", keys_ + ["msk"], ["rsc"], T.rsc[:, 0:n], T.msk[:, 0:n], src, 0.0, A.add, A.max); yield
-            for k, o, c in outs:
-                op("v", "ts", ["rsc", "lc", "bigc"], [k], o, T.rsc[:, 15:n:16], c[0], None, c[1]); yield
+    def both(p, rd, a, b):
+        op("tt", 1, rd, [("mid", p)], part("mid", p), a, b, A.add)
+        op("tt", 1, rd, [("dif", p)], part("dif", p), b, a, A.subtract)
+        centre(p, [p], rd, a)
 
-        minus = (T.bigc[:, 0:1], A.subtract)
-        op("s", "act", [cur, "lo"], ["wl"], T.wl[:], T[cur][:, 0:C].indirect(T.lo[:, 0:1]), F.Copy)
-        yield from part(T.wl[:], ["wl"], 16, [("lo", T.lo[:, 0:1], (T.lc[:, 0:1], A.add))])
-        for lev in range(8):
-            m = 1 << lev
-            if lev < 4:
-                dst, k = (T.wl[:], "wl") if lev < 3 else (T.rw[:, C - 16:C], ("rw", 16))
-                op("s", "act", [cur, cur + "i", "lo"], [k], dst, T[cur][:, 0:2 * C].indirect(T.lo[:, 0:1]), F.Copy)
-                outs = [("lo", T.lo[:, 0:1], (T.lc[:, lev + 1:lev + 2], A.add) if lev < 3 else minus)]
-                if lev == 3:
-                    outs.append(("ro", T.ro[:, 19:20], minus))
-                new = part(dst, [k], 16, outs)
-            if lev >= 4:
-                op("s", "act", [cur, off], [nxt], T[nxt][:, 0:C], T[cur][:, 0:C].indirect(T[off][:]), F.Copy)
-                if lev < 7:
-                    yield from part(T[nxt][:, 0:C], [nxt], C, [("rofs", T.rofs[:], minus)])
-                lst, lk = (T.lo[:, 0:1], "lo") if m == 16 else (T.ro[:, 20 - m // 16:20], "ro")
-                dst, k = T.rw[:, C - 2 * m:C - m], ("rw", 2 * m)
-                op("s", "act", [cur, lk], [k], dst, T[cur][:, 0:C].indirect(lst), F.Copy)
-                new = part(dst, [k], m, [("ro", T.ro[:, 20 - m // 8:20 - m // 16], minus)])
-            if lev < 4:
-                op("s", "act", [cur, off], [nxt], T[nxt][:, 0:C], T[cur][:, 0:C].indirect(T[off][:]), F.Copy)
-            yield from new
-            cur, nxt, off = nxt, cur, "rofs"
-            if lev < 4:
-                yield from part(T[cur][:, 0:C], [cur], C, [("rofs", T.rofs[:], minus)])
-        op("s", "act", [cur, "ro"], [("rw", 320)], T.rw[:, 0:64], T[cur][:, 0:C].indirect(T.ro[:, 16:20]), F.Copy)
-        yield from part(T.rw[:, 0:64], [("rw", 320)], 64, [("ro", T.ro[:, 0:4], minus)])
-        op("v", "set", [], ["km"], T.km[:, 0:1], float(C - 1)); yield
-        op("v", "copy", ["km", "ro"], ["pw"], T.pw[:].indirect(T.ro[:]), T.km[:]); yield
-        op("v", "ts", ["ro"], ["ordo"], T.ordo[:], T.ro[:], -1.0, float(PADZ + C - 1), A.mult, A.add); yield
-        yield from part(T.pw[:], ["pw"], C, [("pmo", T.pmo[:], minus)])
-        op("v", "tt", [("rw", n) for n in (16, 32, 64, 128, 256, 320)] + ["rw2"], ["wd"], T.wd[:], T.rw[:, 0:C], T.rw[:, 1:C + 1], A.subtract); yield
+    def centre(p, ks, rd, now):
+        n = (p[1] - p[0]) // 2
+        op("ts", 2 * n, [("dif", k) for k in ks] + ["bigs"], [("cen", k) for k in ks], part("cen", p), part("dif", p), bigs, None, A.mult)
+        op("tt", n, [("cen", k) for k in ks] + rd, [("cen", k) for k in ks], part("cen", p), part("cen", p), now, A.add)
 
-    def alt(z, le, o):
-        op("v", "tt", [z, "eif"], ["xle"], T.xle[:], T[z][:], T.eif[:], A.is_le); yield
-        op("v", "ts", ["xle"], ["xle"], T.xle[:], T.xle[:], 1000.0, None, A.mult); yield
-        op("v", "tt", ["xle", z], ["xle"], T.xle[:], T.xle[:], T[z][:], A.add); yield
-        op("v", "ts", ["xle"], [o], T[o][:], T.xle[:], float(C), None, A.min); yield
+    both(DI, ["w48"], T.w48[:, 0:24], T.w48[:, 24:48])
+    both(OF, ["z48"], T.z48[:, 0:24], T.z48[:, 24:48])
+    offsets(C, ["bw0"], ["t20"], T.t20[:], "se_", T.bw0[:])
+    both(IV, ["ivin", "t20"], T.ivin[:], T.t20[:])
+    pick("s", C, ["iden", "udo"], ["uw"], T.uw[:], iden, T.udo[:])
+    pick("s", C, ["uw", "mto"], ["umw"], T.umw[:], T.uw[:], T.mto[:])
+    offsets(C, ["umw"], ["t20"], T.t20[:], "se_", T.umw[:])
+    both(UD, ["udin", "t20"], T.udin[:], T.t20[:])
+    KK = [None, (0, 18), (18, 36), (36, 52)]
+    op("iota", 36, [], ["kk"], T.kk[:, 0:36], [[0, 2], [80, 3], [16, 6]], PADZ + 80, 0, **fl)
+    op("iota", 16, [], ["kk3"], T.kk[:, 36:52], [[16, 16]], PADZ + 64, 0, **fl)
+    op("ts", 1, ["kk", "kk3", "pf"], ["kk", "kk3"], T.kk[:, 0:52], T.kk[:, 0:52], pf, 0.25, A.add, A.add)
+    for s in (1, 2, 3):
+        op("ts", 1, ["kk", "kk3", "big"], [("kk", s)], part("kk", KK[s]), part("kk", KK[s]), -K * SIZES[s] / C, big, A.mult, A.subtract)
 
-    def tables():
-        op("s", "act", ["mtw", "ivo"], ["ivmw"], T.ivmw[:], T.mtw[:].indirect(T.ivo[:]), F.Copy)
-        yield from alt("ivs", "xle", "xao")
-        scan("sc", T.ivmw[:], ["ivmw"]); yield
-        op("v", "ts", ["sc", "bigc"], ["t1"], T.t1[:], T.sc[:, 15::16], T.bigc[:, 0:1], None, A.subtract); yield
-        yield from alt("t1", "xle", "xbo")
-        op("v", "tt", ["t1", "ivs"], ["ivd"], T.ivd[:], T.t1[:], T.ivs[:], A.subtract); yield
-        op("s", "act", ["iotc", "iotc2", "xao"], ["xa"], T.xa[:], T.iotc[:, 0:328].indirect(T.xao[:]), F.Copy)
-        op("s", "act", ["iotc", "iotc2", "xbo"], ["xb"], T.xb[:], T.iotc[:, 0:328].indirect(T.xbo[:]), F.Copy)
-        op("v", "tt", ["xa", "iotj"], ["da"], T.da[:], T.xa[:], T.iotj[:], A.subtract); yield
-        op("v", "tt", ["xb", "xa"], ["dd"], T.dd[:], T.xb[:], T.xa[:], A.subtract); yield
-
-    def udtables():
-        op("v", "copy", ["udin"], ["udo"], T.udo[:], T.udin[:]); yield
-        op("v", "copy", ["udin"], ["uds"], T.uds[:], T.udin[:]); yield
-        op("s", "act", ["iotj", "udo"], ["xa"], T.xa[:], T.iotj[:].indirect(T.udo[:]), F.Copy)
-        op("s", "act", ["xa", "mto"], ["xb"], T.xb[:], T.xa[:].indirect(T.mto[:]), F.Copy)
-        scan("sce", T.xb[:], ["xb"]); yield
-        op("v", "ts", ["sce", "bigc"], ["sn"], T.sn[:], T.sce[:, 15::16], T.bigc[:, 0:1], None, A.subtract); yield
-        op("v", "tt", ["sn", "uds"], ["udd"], T.udd[:], T.sn[:], T.uds[:], A.subtract); yield
-
-    def run(main, *side):
-        side = [s for s in side]
-        for _ in main:
-            while side:
-                try:
-                    next(side[0])
-                    break
-                except StopIteration:
-                    side.pop(0)
-        for s in side:
-            for _ in s:
-                pass
-
-    def quantise_x(k, tile):
-        op("v", "quant", [tile], ["qx%d" % k, "sx%d" % k], T["qx%d" % k][:], T["sx%d" % k][:], T[tile][:])
-
-    def mm(bank, w, ws, x, xs, wv, wsv, xv, xsv, n):
-        op("t", "mm", [w, ws, x, xs], ["ps%d" % bank], T["ps%d" % bank][:, 0:n], wv, wsv, xv, xsv, True, True)
-
-    def unpack(bank, i, qn, sn):
-        mm(bank, "qe%d" % i, "se%d" % i, qn, sn, T.qe[:, 128 * i:128 * i + 128], T.se[:, 128 * i:128 * i + 128], T[qn][:], T[sn][:], C)
-
-    def th_copy(dst, i, bank):
-        op("s", "act", ["ps%d" % bank], [(dst, i)], T[dst][:, C * i:C * i + C], T["ps%d" % bank][:, 0:C], F.Copy, scale=0.5)
-
-    def pick(dst, src, i, off):
-        op("s", "act", [(src, i), off], [(dst, i)], T[dst][:, C * i:C * i + C], T[src][:, C * i:C * i + C].indirect(li(off)), F.Copy)
+    quant(C, ["xin"], ["qx0"], T.qx0[:], T.sx0[:], T.xin[:])
+    quant(128, ["uin"], ["qu"], T.qu[:], T.su[:], T.uin[:])
+    op("iota", 8, [], ["c8"], T.c8[:], [[16, 8]], 0, 0)
+    op("copy", 1, ["c8"], ["uof"], T.uof[:], T.c8[:])
+    op("copy", 128, ["qu", "uof"], ["qr"], T.qr[:].bitcast(dt.uint32), T.qu[:].bitcast(dt.uint32).indirect(T.uof[:]), kind="gather")
+    pick("s", 128, ["qu", "uof"], ["sr"], T.sr[:], T.su[:], T.uof[:])
+    quant(128, ["vin"], ["qv"], T.qv_[:], T.sv[:], T.vin[:])
 
     OWNB, PARB = [1, 2, 3, 4], [5, 6, 7, 0]
 
-    def keys(s, sets):
-        return [("d%d" % s, k) for k in sets]
+    def unpack(dst, banks, qn, sn, rd):
+        for i in range(4):
+            mm(banks[i], C, [("qe", i)] + rd, T.qe[:, 128 * i:128 * i + 128], T.se[:, 128 * i:128 * i + 128], T[qn][:], T[sn][:])
+            op("act", C, ["ps%d" % banks[i]], [(dst, i)], T[dst][:, C * i:C * i + C], T["ps%d" % banks[i]][:, 0:C], F.Copy, scale=0.5)
 
-    def stage(s):
-        w = C // RAD[s]
-        nb = C // SIZES[s]
-        if w // 16 % 2:
-            op("v", "ts", ["t1"], ["ob"], T.ob[:, 1:21], T.t1[:], -float(nb), None, A.mult); yield
-        op("v", "ts", ["t1"], ["oa"], T.oa[:, 0:20], T.t1[:], -float(nb), None, A.mult); yield
+    def edit(r, ps, views):
+        lst, whole = "lst%d" % r, (ps[0][0], ps[-1][1])
+        for p, (rd, v) in zip(ps, views):
+            op("tt", 1, rd + [("dif", p)], [("mul", p)], part("mul", p), v, part("dif", p), A.mult)
+        op("tt", 24 * len(ps), [(n, p) for n in ("mul", "cen") for p in ps], [("val", p) for p in ps], part("val", whole), part("mul", whole), part("cen", whole), A.add)
+        op("copy", 1, [("val", p) for p in ps], [(lst, p) for p in ps], part(lst, whole), part("val", whole))
+
+    def stage(s, off, offk, cols, src, srck):
+        w, d = C // RAD[s], T["d%d" % s]
         for k in range(1, RAD[s]):
-            c0 = k * w // 16
-            o, lo = ("oa", c0) if c0 % 2 == 0 else ("ob", c0 + 1)
-            d = T["d%d" % s]
-            lim = PADZ + k * w
-            op("v", "tt", keys(s, range(-1, k + 1)) + [o], keys(s, [k]), d[:, lim:lim + w], d[:, 0:lim].indirect(T[o][:, lo:lo + w // 16]), d[:, lim:lim + w], A.add); yield
-
-    def turn(s):
-        q = RAD[s + 1]
-        w = C // q
-        src, o, ks = (T.da, 0, ["da"]) if s < 0 else (T["d%d" % s], PADZ, keys(s, range(RAD[s])))
-        for i in range(q):
-            v = src[:, o + q - 1 - i:o + C:q]
-            op("v", "scan", ks + ["msk"], [("sc", i)] + (["sc"] if i == 0 else []), T.sc[:, w * i:w * i + w], T.msk[:, 0:w], v, 0.0, A.add, A.max); yield
-            op("s", "act", ks, keys(s + 1, [i]), T["d%d" % (s + 1)][:, PADZ + w * i:PADZ + w * i + w], v, F.Copy)
-        k = "k%d" % (s + 1)
-        op("v", "tt", [("sc", i) for i in range(q)] + ["sc", k], ["t1"], T.t1[:], T.sc[:, 15::16], T.kk[:, 20 * s + 20:20 * s + 40], A.add); yield
-
-    def edit_iv(r):
-        op("v", "scan", ["giv", "msks"], ["scs"], T.scs[:], T.msks[:], T.giv[:], 0.0, A.add, A.max); yield
-        op("v", "ts", ["scs", "bigs"], ["sf"], T.sf[:], T.scs[:, 15::16], T.bigs[:, 0:1], None, A.subtract); yield
-        op("v", "tt", ["sf", "ivd"], ["sm"], T.sm[:], T.sf[:], T.ivd[:], A.mult); yield
-        op("v", "tt", ["ivs", "sm"], ["ivs"], T.ivs[:], T.ivs[:], T.sm[:], A.add); yield
-        op("v", "copy", ["ivs"], ["ivn%d" % r], li("ivn%d" % r), T.ivs[:])
-        send(rank ^ STEP[r], "ivn%d" % r, li("ivp%d" % r), li("ivn%d" % r), "ai%d" % r); yield
-        if r < 2:
-            op("v", "ts", ["sm"], ["sn"], T.sn[:], T.sm[:], -2.0, None, A.mult); yield
-            op("v", "tt", ["ivd", "sn"], ["ivd"], T.ivd[:], T.ivd[:], T.sn[:], A.add); yield
-
-    def edit_ud(r):
-        op("v", "scan", ["sw", "msks"], ["scs"], T.scs[:], T.msks[:], T.sw[:], 0.0, A.add, A.max); yield
-        op("v", "ts", ["scs", "bigs"], ["sf"], T.sf[:], T.scs[:, 15::16], T.bigs[:, 0:1], None, A.subtract); yield
-        op("v", "tt", ["sf", "udd"], ["sm"], T.sm[:], T.sf[:], T.udd[:], A.mult); yield
-        op("v", "tt", ["uds", "sm"], ["uds"], T.uds[:], T.uds[:], T.sm[:], A.add); yield
-        op("v", "copy", ["uds"], ["udn"], T.udn[:], T.uds[:]); yield
-        if r < 2:
-            op("v", "ts", ["sm"], ["sn"], T.sn[:], T.sm[:], -2.0, None, A.mult); yield
-            op("v", "tt", ["udd", "sn"], ["udd"], T.udd[:], T.udd[:], T.sn[:], A.add); yield
-
-    def signs(r):
-        ivo = "ivo" if r == 0 else "ivn%d" % (r - 1)
-        op("v", "ts", ["ps0"], ["pp"], T.pp[:], T.ps0[:, 0:C], 0.0, None, A.is_le); yield
-        op("s", "act", ["ps5"], ["sg"], T.sg[:], T.ps5[:, 0:C], F.Sign)
-        op("v", "tt", ["pp", "mto", "sg"], ["sw"], T.sw[:], T.pp[:].indirect(T.mto[:]), T.sg[:], A.is_lt); yield
-        op("s", "act", ["sw", ivo], ["giv"], T.giv[:], T.sw[:].indirect(li(ivo)), F.Copy)
-        op("v", "tt", ["sw", ivo, "dd"], ["tt"], T.tt[:], T.sw[:].indirect(li(ivo)), T.dd[:], A.mult); yield
-        op("v", "tt", ["tt", "da"], ["da"], T.da[:], T.da[:], T.tt[:], A.add); yield
-        yield from turn(-1)
-
-    def undos(r):
-        qp, sp = "qp%d" % r, "sp%d" % r
-        th_copy("th", 0, OWNB[0])
-        th_copy("th", 1, OWNB[1])
-        yield from stage(0)
-        yield from turn(0)
-        th_copy("th", 2, OWNB[2])
-        th_copy("th", 3, OWNB[3])
-        yield from stage(1)
-        yield from turn(1)
-        for i in range(4):
-            unpack(PARB[i], i, qp, sp)
-        yield from stage(2)
-        yield from turn(2)
-        for i in range(4):
-            th_copy("thp", i, PARB[i])
-        yield from stage(3)
-        for i in range(4):
-            pick("tiv", "thp", i, "ivp%d" % r)
-
-    def bypass(r):
-        op("v", "ts", keys(3, range(-1, 5)) + ["ordo"], ["vi"], T.vi[:], T.d3[:, 0:PADZ + C].indirect(T.ordo[:]), 1024.0, None, A.mult); yield
-        op("v", "ts", ["vi"], ["vi"], T.vi[:], T.vi[:], 1, None, A.bitwise_and); yield
-        op("v", "scan", ["vi", "wd"], ["st"], T.st[:], T.vi[:], T.wd[:], 0.0, A.mult, A.add); yield
-        op("v", "tt", ["st", "pmo", "iotj"], ["bw"], T.bw[:], T.st[:].indirect(T.pmo[:]), T.iotj[:], A.add); yield
-        scan("sce", T.bw[:], ["bw"]); yield
-        op("v", "ts", ["sce", "bigc"], ["bn%d" % r], li("bn%d" % r), T.sce[:, 15::16], T.bigc[:, 0:1], None, A.subtract)
-        send(rank ^ STEP[r], "bn%d" % r, li("bp%d" % r), li("bn%d" % r), "ab%d" % r); yield
-
-    def partner_e(r):
-        op("s", "act", ["bw", "ivp%d" % r], ["ew"], T.ew[:], T.bw[:].indirect(li("ivp%d" % r)), F.Copy)
-        yield from edit_ud(r)
-        scan("sce", T.ew[:], ["ew"]); yield
-        op("v", "ts", ["sce", "bigc"], ["en%d" % r], li("en%d" % r), T.sce[:, 15::16], T.bigc[:, 0:1], None, A.subtract)
-        send(rank ^ STEP[r], "en%d" % r, li("ep%d" % r), li("en%d" % r), "ae%d" % r); yield
-
-    def flat(*gens):
-        for x in gens:
-            yield from x
-
-    def prepare():
-        quantise_x(0, "xin"); yield
-        op("v", "quant", ["uin"], ["qu", "su"], T.qu[:], T.su[:], T.uin[:])
-        op("v", "copy", ["c16"], ["uof"], T.uof[:], T.c16[:, 0:8])
-        op("v", "copy", ["qu", "uof"], ["qr"], T.qr[:].bitcast(dt.uint32), T.qu[:].bitcast(dt.uint32).indirect(T.uof[:]))
-        op("s", "act", ["su", "uof"], ["sr"], T.sr[:], T.su[:].indirect(T.uof[:]), F.Copy)
-
-    def constants():
-        for i in range(4):
-            op("v", "quant", ["eb"], ["qe%d" % i, "se%d" % i], T.qe[:, 128 * i:128 * i + 128], T.se[:, 128 * i:128 * i + 128], T.eb[:, 3 - i:3 - i + 512]); yield
-
-    def exchange(r):
-        p = rank ^ STEP[r]
-        qx, sx = "qx%d" % r, "sx%d" % r
-        send(p, qx, T["qp%d" % r][:].bitcast(dt.uint8), T[qx][:].bitcast(dt.uint8), "aq%d" % r)
-        send(p, sx, T["sp%d" % r][:], T[sx][:], "as%d" % r); yield
-        for bank in (0, 5):
-            mm(bank, "qr", "sr", qx, sx, T.qr[:], T.sr[:], T[qx][:], T[sx][:], C)
-
-    def own(r):
-        for i in range(4):
-            unpack(OWNB[i], i, "qx%d" % r, "sx%d" % r); yield
+            lim, c0 = PADZ + k * w, cols * (k - 1)
+            op("tt", w, [("d%d" % s, i) for i in range(-1, k)] + [offk] + srck(k), [("d%d" % s, k)], d[:, lim:lim + w],
+               d[:, 0:lim].indirect(off[:, c0:c0 + w // 16] if s else T[off[0]][:, off[1] + c0:off[1] + c0 + w // 16]), src(k), A.add, kind="gather")
 
     for r in range(3):
-        if r == 0:
-            merge(chain(ring()),
-                  chain(prepare(), exchange(0), ("mark", "x"), constants(), own(0), ("mark", "own")),
-                  chain(places(), tables(), places2(), ("after", "x"), signs(0), ("mark", "giv"), ("after", "own"), undos(0)),
-                  chain(("after", "giv"), edit_iv(0), udtables()))
-        else:
-            merge(chain(exchange(r), own(r), signs(r), ("mark", "giv"), undos(r)), chain(("after", "giv"), edit_iv(r)))
-        for _ in bypass(r):
-            pass
-        for _ in partner_e(r):
-            pass
-        for i in range(4):
-            pick("tu", "th", i, "udn")
-        if r < 2:
-            op("s", "act", ["tt"], ["sg"], T.sg[:], T.tt[:], F.Copy, scale=-2.0)
-        else:
-            op("s", "act", ["iotj", "udn"], ["xa"], T.xa[:], T.iotj[:].indirect(T.udn[:]), F.Copy)
-            dma("y", "duo", ["xa"], [], T.uo[:, :], T.xa[0:128:16, :])
-            op("v", "quant", ["vin"], ["qv_", "sv"], T.qv_[:], T.sv[:], T.vin[:])
+        qx, sx, qp, sp, lst = "qx%d" % r, "sx%d" % r, "qp%d" % r, "sp%d" % r, "lst%d" % r
+        ivp, bn, bp, en, ep = ["%s%d" % (n, r) for n in ("ivp", "bn", "bp", "en", "ep")]
+        send(r, [qx], qp, T[qp][:].bitcast(dt.uint8), T[qx][:].bitcast(dt.uint8), "aq%d" % r, 4.0)
+        send(r, [qx], sp, T[sp][:], T[sx][:], "as%d" % r, 5.0)
+        mm(0, C, ["qr", "sr", qx], T.qr[:], T.sr[:], T[qx][:], T[sx][:])
+        op("ts", C, ["ps0"], ["np"], T.np_[:], T.ps0[:, 0:C], 0.0, None, A.is_le)
         for h in range(2):
+            a = H * h
+            mm(5 + h, H, ["qr", "sr", qx], T.qr[:], T.sr[:], T[qx][:, a:a + H], T[sx][:, a:a + H])
+            op("act", H, ["ps%d" % (5 + h)], [("sg", h)], T.sg[:, a:a + H], T["ps%d" % (5 + h)][:, 0:H], F.Sign)
+            op("tt", H, ["np", ("sg", h), "mto"], [("sw", h)], T.sw[:, a:a + H], T.np_[:].indirect(T.mto[:, 10 * h:10 * h + 10]), T.sg[:, a:a + H], A.is_lt, kind="gather")
+        sw = [("sw", 0), ("sw", 1)]
+        for h, q in enumerate("vs"):
+            pick(q, H, sw + ["ivo"], [("sa", h)], T.sa[:, H * h:H * h + H], T.sw[:], T.ivo[:, 10 * h:10 * h + 10])
+        sa = [("sa", 0), ("sa", 1)]
+        for k in range(4):
+            scans(80, sa, [("scs", k)], T.scs[:, 96 * k:96 * k + 80], T.sa[:, 3 - k::4])
+        edit(r, [DI, OF], [([("scs", k) for k in range(4)], T.scs[:, 15::16])] * 2)
+        scans(C, sa, [("scn", 0)], T.scn[:, 0:C], T.sa[:])
+        scans(C, sw, [("scn", 1)], T.scn[:, C:2 * C], T.sw[:])
+        edit(r, [IV], [([("scn", 0)], T.scn[:, 15:C:16])])
+        edit(r, [UD], [([("scn", 1)], T.scn[:, C + 15::16])])
+        send(r, [(lst, IV)], ivp, li(ivp), part(lst, IV), "ai%d" % r)
+        if r < 2:
+            ps = [DI, OF, IV, UD]
+            op("ts", 88, [("val", p) for p in ps], [("dif", p) for p in ps], T.dif[:], T.val[:], -2.0, None, A.mult)
+            op("tt", 88, [(n, p) for n in ("dif", "mid") for p in ps], [("dif", p) for p in ps], T.dif[:], T.dif[:], T.mid[:], A.add)
+            centre(ALL, ps, [("val", p) for p in ps], T.val[:])
+        unpack("th", OWNB, qx, sx, [qx])
+        for k, q in enumerate("svss"):
+            out, key = (T.d0[:, PADZ:PADZ + 80], ("d0", 0)) if k == 0 else (T.e0[:, 80 * k:80 * k + 80], ("e0", k))
+            pick(q, 80, ["tab", (lst, DI)], [key], out, T.tab[:], T[lst][:, 6 * k:6 * k + 5])
+        stage(0, (lst, OF[0] + 6), (lst, OF), 6, lambda k: T.e0[:, 80 * k:80 * k + 80], lambda k: [("e0", k)])
+        for s in (1, 2, 3):
+            q, was = RAD[s], "d%d" % (s - 1)
+            w, ks = C // q, [(was, i) for i in range(RAD[s - 1])]
+            cols = 6 if w == 80 else 4
+
+            def view(k, q=q, was=was):
+                return T[was][:, PADZ + q - 1 - k:PADZ + C:q]
+            for k in range(1, q):
+                scan(w, ks, [("sc", k)], T.sc[:, 16 * cols * (k - 1):16 * cols * (k - 1) + w], view(k))
+            n = cols * (q - 1)
+            op("tt", 1, [("sc", k) for k in range(1, 5)] + [("kk", s)], ["t1"], T.t1[:, 0:n], T.sc[:, 15:16 * n:16], part("kk", KK[s]), A.add)
+            op("copy", w, ks, [("d%d" % s, 0)], T["d%d" % s][:, PADZ:PADZ + w], view(0))
+            op("ts", 1, ["t1"], ["oa"], T.oa[:, 0:n], T.t1[:, 0:n], -C / SIZES[s] / K, None, A.mult)
+            stage(s, T.oa, "oa", cols, view, lambda k, ks=ks: ks)
+        unpack("thp", PARB, qp, sp, [qp, sp])
+        for i in range(4):
+            pick("s", C, [("thp", i), ivp], [("tiv", i)], T.tiv[:, C * i:C * i + C], T.thp[:, C * i:C * i + C], li(ivp))
+        op("ts", C, [("d3", i) for i in range(-1, 5)] + ["ordo"], ["ne"], T.ne[:], T.d3[:].indirect(T.ordo[:]), 1, None, A.bitwise_and, kind="gather")
+        op("scan", C, ["ne", "wd"], ["st"], T.st[:], T.ne[:], T.wd[:], 0.0, A.mult, A.add)
+        for h in range(2):
+            a, c = H * h, 10 * h
+            op("tt", H, ["st", "pmo", "iden"], [("bw", h)], T.bw[:, a:a + H], T.st[:].indirect(T.pmo[:, c:c + 10]), T.iden[:, a:a + H], A.add, kind="gather")
+            offsets(H, [("bw", h)], [(bn, h)], li(bn, c, 10), ("sb", "rsc")[h], T.bw[:, a:a + H])
+            send(r, [(bn, h)], (bp, h), li(bp, c, 10), li(bn, c, 10), ("ab%d", "ac%d")[h] % r)
+        pick("s", C, [("bw", 0), ("bw", 1), ivp], ["ew"], T.ew[:], T.bw[:], li(ivp))
+        offsets(C, ["ew"], [en], li(en), "se_", T.ew[:])
+        send(r, [en], ep, li(ep), li(en), "ae%d" % r)
+        for i in range(4):
+            pick("s", C, [("th", i), (lst, UD)], [("tu", i)], T.tu[:, C * i:C * i + C], T.th[:, C * i:C * i + C], part(lst, UD))
+        if r == 2:
+            pick("s", C, ["iden", (lst, UD)], ["uw"], T.uw[:], iden, part(lst, UD))
+            dma("y", "duo", ["uw"], [], T.uo[:, :], T.uw[0:128:16, :])
+        for h in range(2):
+            a, c = H * h, 10 * h
             for i in range(4):
-                c0 = 160 * h
-                op("v", "tt", [("thp", i), ("tiv", i), "bp%d" % r], [("zt", h, i)], T.zt[:, 4 * c0 + i:4 * c0 + 640:4],
-                   T.thp[:, C * i:C * i + C].indirect(li("bp%d" % r, 10 * h, 10 * h + 10)), T.tiv[:, C * i + c0:C * i + c0 + 160], A.add)
-            op("v", "quant", [("zt", h, i) for i in range(4)], ["qz%d" % h, "sz%d" % h], T.qz[:, 160 * h:160 * h + 160], T.sz[:, 160 * h:160 * h + 160], T.zt[:, 640 * h:640 * h + 640])
+                op("tt", H, [("thp", i), ("tiv", i), (bp, h)], [("zt", h, i)], T.zt[:, 4 * a + i:4 * a + 4 * H:4],
+                   T.thp[:, C * i:C * i + C].indirect(li(bp, c, 10)), T.tiv[:, C * i + a:C * i + a + H], A.add, kind="gather")
+            quant(H, [("zt", h, i) for i in range(4)], [("qz", h)], T.qz[:, a:a + H], T.sz[:, a:a + H], T.zt[:, 4 * a:4 * a + 4 * H])
             for i in range(4):
                 bank = (OWNB, PARB)[h][i]
-                mm(bank, "qw", "sw_", "qz%d" % h, "sz%d" % h, T.qw[:, 128 * i:128 * i + 128], T.sw_[:, 128 * i:128 * i + 128], T.qz[:, 160 * h:160 * h + 160], T.sz[:, 160 * h:160 * h + 160], 160)
-                op("s", "act", ["ps%d" % bank], [("hh", i, h)], T.hh[:, C * i + 160 * h:C * i + 160 * h + 160], T["ps%d" % bank][:, 0:160], F.Copy, scale=2.0 ** -6)
-        if r < 2:
-            op("v", "tt", ["dd", "sg"], ["dd"], T.dd[:], T.dd[:], T.sg[:], A.add)
-        for i in range(4):
-            op("v", "tt", [("hh", i, 0), ("hh", i, 1), ("tu", i), "ep%d" % r], [("xt", i)], T.xt[:, i::4],
-               T.hh[:, C * i:C * i + C].indirect(li("ep%d" % r)), T.tu[:, C * i:C * i + C], A.add)
-        n = r + 1
-        op("v", "quant", [("xt", i) for i in range(4)], ["qx%d" % n, "sx%d" % n], T["qx%d" % n][:], T["sx%d" % n][:], T.xt[:])
-
-    dma("y", "doc", ["qx3"], [], T.oc[:], T.qx3[:].bitcast(dt.uint8))
+                mm(bank, H, ["qw", "sw_", ("qz", h)], T.qw[:, 128 * i:128 * i + 128], T.sw_[:, 128 * i:128 * i + 128], T.qz[:, a:a + H], T.sz[:, a:a + H])
+                op("act", H, ["ps%d" % bank], [("hh", i, h)], T.hh[:, C * i + a:C * i + a + H], T["ps%d" % bank][:, 0:H], F.Copy, scale=2.0 ** -6)
+        qn, sn = "qx%d" % (r + 1), "sx%d" % (r + 1)
+        for h, (a, n) in enumerate(((0, C),) if r < 2 else ((0, H), (H, H))):
+            for i in range(4):
+                op("tt", n, [("hh", i, 0), ("hh", i, 1), ("tu", i), ep], [("xt", i, h)] + ([("xt", i, 1)] if n == C else []), T.xt[:, 4 * a + i:4 * (a + n):4],
+                   T.hh[:, C * i:C * i + C].indirect(li(ep, a // 16, n // 16)), T.tu[:, C * i + a:C * i + a + n], A.add, kind="gather")
+            key = qn if r < 2 else (qn, h)
+            quant(n, [("xt", i, h) for i in range(4)], [key], T[qn][:, a:a + n], T[sn][:, a:a + n], T.xt[:, 4 * a:4 * (a + n)])
+            if r == 2:
+                dma("y", "doc%d" % h, [key], [], T.oc[:, 4 * a:4 * (a + n)], T[qn][:, a:a + n].bitcast(dt.uint8), 2.5)
+                mm(1 + h, n, ["qv", key], T.qv_[:], T.sv[:], T[qn][:, a:a + n], T[sn][:, a:a + n])
+                op("act", n, ["ps%d" % (1 + h)], [("ys", h)], T.ys[:, a:a + n], T["ps%d" % (1 + h)][:, 0:n], F.Copy)
+                dma("s", "dy%d" % h, [("ys", h)], [], T.y[:, a:a + n], T.ys[:, a:a + n], 2.5)
     for k in range(4):
-        dma("s" if k < 2 else "y", "ds%d" % k, ["sx3"], [], T.osc[4 * k:4 * k + 4, :], T.sx3[32 * k:32 * k + 4, :])
-    mm(0, "qv_", "sv", "qx3", "sx3", T.qv_[:], T.sv[:], T.qx3[:], T.sx3[:], C)
-    op("v", "copy", ["ps0"], ["ys"], T.ys[:], T.ps0[:, 0:C])
-    dma("y", "dy0", ["ys"], [], T.y[:], T.ys[:])
-    for s, n in total.items():
+        dma("y", "ds%d" % k, [("qx3", 0), ("qx3", 1)], [], T.osc[4 * k:4 * k + 4, :], T.sx3[32 * k:32 * k + 4, :])
+
+    token, seen = {}, {q: {} for q in eng}
+    for i in order(calls):
+        q, need = calls[i]["q"], {}
+        for d in calls[i]["deps"]:
+            s, n = token[d]
+            need[s] = max(need.get(s, 0), n)
+        for s, n in need.items():
+            if seen[q].get(s, 0) < n:
+                eng[q].wait_ge(T.sem[s], n)
+                seen[q][s] = n
+        token[i] = calls[i]["issue"]()
+    for s, n in count.items():
         g.wait_ge(T.sem[s], n)

from concourse.mybir import dt, AluOpType as A, ActivationFunctionType as F

C = 320
H = C // 2
RAD = [4, 4, 4, 5]
SIZES = [4, 16, 64, 320]
STEP = [1, 2, 4]
PADZ = 16
K = 1024.0
BIG, LOW = 2.0 ** 20, -2.0 ** 22
BIGS = 4.0
F4, U8, BF, F32, I32, U16 = "float8_e4m3fn_x4", "uint8", "bfloat16", "float32", "int32", "uint16"
DI, OF, IV, UD, ALL = (0, 24), (24, 48), (48, 68), (68, 88), (0, 88)

SCRATCH = {}
SEMAPHORES = ["qv", "qs", "qt", "qg", "sent"]


def _buf(name, n, dtype):
    SCRATCH[name] = ("sbuf", [128, n], dtype)


for _n in ("ud", "iv", "hp", "mt"):
    _buf(_n + "in", 20, I32)
    _buf(_n + "o", 20, U16)
    SEMAPHORES.append("d" + _n)
for _n in ("x", "u", "v", "wc", "ws", "y0", "y1", "oc0", "oc1", "s0", "s1", "s2", "s3", "uo"):
    SEMAPHORES.append("d" + _n)
for _n, _w, _t in (("xin", 1280, BF), ("uin", 512, BF), ("vin", 512, BF), ("eb", 520, BF), ("ones", 520, BF),
                   ("pw", 10 * C, F32), ("iden", C, F32), ("tab", C, F32), ("ti", 16, I32), ("pa", 20, I32), ("po", 20, U16), ("m16", 32, F32),
                   ("msk", C, F32), ("msks", C, BF), ("col", 8, F32), ("ci", 4, I32), ("c8", 8, I32), ("uof", 8, U16),
                   ("jj", 48, F32), ("pp", 48, F32), ("kk", 56, F32), ("d48", 48, F32), ("z48", 48, F32), ("w48", 48, F32), ("t20", 20, F32),
                   ("mtw", C, F32), ("aw", C, F32), ("bw0", C, F32), ("uw", C, F32), ("umw", C, F32), ("sab", 768, F32),
                   ("ro4", 20, U16), ("ro16", 20, U16), ("x0", 2, U16), ("x1", 2, U16), ("lo", 2, U16), ("wl", 16, F32), ("rsc", C, F32),
                   ("ro", 20, U16), ("rw", 328, F32), ("km", C, F32), ("pm", C, F32), ("pmo", 20, U16), ("wd", C, F32), ("ordo", 20, U16),
                   ("mid", 88, F32), ("dif", 88, F32), ("cen", 88, F32), ("mul", 88, F32), ("val", 88, F32),
                   ("sg", C, BF), ("np_", C, BF), ("sw", C, BF), ("sa", C, BF), ("scs", 384, BF), ("scn", 2 * C, BF), ("e0", C, F32),
                   ("sc", 288, F32), ("t1", 18, F32), ("oa", 18, U16), ("ne", C, I32), ("st", C, F32), ("bw", C, F32), ("ew", C, F32),
                   ("sb", C, F32), ("se_", C, F32),
                   ("th", 1280, BF), ("thp", 1280, BF), ("tiv", 1280, BF), ("tu", 1280, BF), ("hh", 1280, BF), ("xt", 1280, BF), ("zt", 1280, BF),
                   ("ys", C, F32),
                   ("qu", 128, F4), ("su", 128, U8), ("qr", 128, F4), ("sr", 128, U8), ("qv_", 128, F4), ("sv", 128, U8),
                   ("qw", 512, F4), ("sw_", 512, U8), ("qe", 512, F4), ("se", 512, U8), ("qz", C, F4), ("sz", C, U8)):
    _buf(_n, _w, _t)
for _i in range(4):
    _buf("d%d" % _i, PADZ + C, I32 if _i == 3 else F32)
    _buf("qx%d" % _i, C, F4)
    _buf("sx%d" % _i, C, U8)
for _i in range(3):
    _buf("qp%d" % _i, C, F4)
    _buf("sp%d" % _i, C, U8)
    _buf("lst%d" % _i, 128, U16)
    _buf("land%d" % _i, 72, U16)
    SEMAPHORES += ["%s%d" % (_n, _i) for _n in ("aq", "as", "ai", "ab", "ac", "ae")]
for _i in range(8):
    SCRATCH["ps%d" % _i] = ("psum", [128, 512], F32)

WAKE = 0.06
CFG = {"split": 0, "wait": 0.5, "passes": 3}


def lasts(name, n, kind):
    if kind == "gather":
        return 0.06 + 0.0016 * n
    if kind == "scatter":
        return 0.06 + 0.004 * n
    if name == "quant":
        return 0.015 + 0.0011 * n
    if name == "mm":
        return 0.0006 * (n + 16)
    if name in ("iota", "sel"):
        return 0.16 + 0.0021 * n
    return max(0.067, n * (0.0021 if name == "tt" else 0.00052 if kind == "short" else 0.00104))


def order(calls):
    n = len(calls)
    after = [[] for c in calls]
    for i, c in enumerate(calls):
        for d in c["deps"]:
            after[d].append(i)

    def place(urge, back):
        before, behind = (after, [c["deps"] for c in calls]) if back else ([c["deps"] for c in calls], after)
        left, free, begin = [len(b) for b in before], {}, {}
        ready = {i: calls[i]["lat"] * back for i in range(n) if not left[i]}
        while ready:
            est = {i: max(t, free.get(calls[i]["q"], 0.0)) for i, t in ready.items()}
            j = min(est, key=lambda i: (est[i] + calls[i]["dur"], i))
            near = [i for i in est if calls[i]["q"] == calls[j]["q"]]
            first = min(est[i] for i in near)
            i = max((i for i in near if est[i] <= first + CFG["wait"] * (est[j] + calls[j]["dur"] - first)), key=lambda i: (urge[i], -i))
            begin[i], free[calls[i]["q"]] = est[i], est[i] + calls[i]["dur"]
            del ready[i]
            for d in behind[i]:
                left[d] -= 1
                if not left[d]:
                    ready[d] = calls[d]["lat"] * back + max(begin[k] + calls[k]["dur"] + calls[k]["lat"] * (not back) + WAKE for k in before[d])
        return [begin[i] + calls[i]["dur"] for i in range(n)], begin

    urge = [0.0] * n
    for i in reversed(range(n)):
        urge[i] = calls[i]["dur"] + calls[i]["lat"] + max([0.0] + [urge[d] + WAKE for d in after[i]])
    best = None
    for _ in range(CFG["passes"]):
        ends, begin = place(urge, False)
        end = max(ends[i] + calls[i]["lat"] for i in range(n))
        if best is None or end < best[0]:
            best = (end, begin)
        urge = place(ends, True)[0]
    CFG["est"] = best[0]
    return sorted(range(n), key=lambda i: (best[1][i] if calls[i]["deps"] or not calls[i]["lat"] else 0.0, i))


def rank_program(g, core, T, topo):
    rank = T.rank_of(core)
    if rank is None:
        return
    V, S, P, Y = g.vector, g.scalar, g.tensor, g.sync
    eng = {"v": V, "s": S, "t": P, "g": g, "y": Y}
    fns = {"copy": V.tensor_copy, "tt": V.tensor_tensor, "ts": V.tensor_scalar, "scan": V.tensor_tensor_scan, "set": V.memset,
           "quant": V.quantize_mx, "act": S.activation, "mm": P.matmul_mx, "iota": g.iota, "sel": g.affine_select}
    calls, lastw, readers = [], {}, {}

    def note(q, rd, wr, dur, lat, issue):
        deps = {lastw[k] for k in rd}
        for k in wr:
            deps.update(readers.get(k, []) + ([lastw[k]] if k in lastw else []))
        for k in rd:
            readers.setdefault(k, []).append(len(calls))
        for k in wr:
            lastw[k], readers[k] = len(calls), []
        calls.append({"q": q, "deps": deps, "dur": dur, "lat": lat, "issue": issue})

    count = {}

    def op(name, n, rd, wr, *a, kind="", **kw):
        q = {"act": "s", "mm": "t", "iota": "g", "sel": "g"}.get(name, "v")

        def issue():
            count["q" + q] = count.get("q" + q, 0) + 1
            fns[name](*a, **kw).then_inc(T.sem["q" + q], 1)
            return "q" + q, count["q" + q]
        note(q, rd, wr, lasts(name, n, kind), 0.0, issue)

    def dma(q, sem, rd, wr, out, in_, lat=2.0):
        def issue():
            count[sem] = 16
            eng[q].dma_start(out, in_).then_inc(T.sem[sem], 16)
            return sem, 16
        note(q, rd, wr, 0.05, lat, issue)

    def send(r, key, land, out, in_, sem, lat=2.1):
        dst = T.cores[rank ^ STEP[r]]

        def issue():
            rid, pid = topo.addr(dst)[:2]
            count["sent"] = count.get("sent", 0) + len(topo.engines(core, dst))
            count[sem] = len(topo.engines(dst, core))
            g.remote_dma(out, in_, T.sem[sem], T.sem.sent, pid, rid, topo.mask(core, dst))
            return sem, count[sem]
        note("g", key, [land], 0.1, lat, issue)

    def pick(q, n, rd, wr, out, win, off, **kw):
        if q == "s":
            op("act", n, rd, wr, out, win.indirect(off), F.Copy, kind="gather", **kw)
        else:
            op("copy", n, rd, wr, out, win.indirect(off), kind="gather")

    def scan(n, rd, wr, out, src):
        op("scan", n, rd + ["msk"], wr, out, T.msk[:, 0:n], src, 0.0, A.add, A.max)

    def scans(n, rd, wr, out, src):
        op("scan", n, rd + ["msks"], wr, out, T.msks[:, 0:n], src, 0.0, A.add, A.max, kind="short")

    def offsets(n, rd, wr, out, buf, src, add=None):
        scan(n, rd, [buf], T[buf][:, 0:n], src)
        if add is None:
            op("ts", 1, [buf, "big"], wr, out, T[buf][:, 15:n:16], big, None, A.subtract)
        else:
            op("ts", 1, [buf, add[0]], wr, out, T[buf][:, 15:n:16], add[1], None, A.add)

    def quant(n, rd, wr, q, s, t):
        op("quant", n, rd, wr, q, s, t)

    def mm(bank, n, rd, w, ws, x, xs):
        op("mm", n, rd, ["ps%d" % bank], T["ps%d" % bank][:, 0:n], w, ws, x, xs, True, True)

    def part(buf, p):
        return T[buf][:, p[0]:p[1]]

    def li(name, c=0, n=20):
        buf, o = {"bn": ("lst", 88), "en": ("lst", 108), "ivp": ("land", 0), "bp": ("land", 24), "ep": ("land", 48)}[name[:-1]]
        return T[buf + name[-1]][:, o + c:o + c + n]

    big, bigs, pf, slot = T.col[:, 0:1], T.col[:, 1:2], T.col[:, 2:3], T.col[:, 3:4]
    iden = T.iden[:]

    dma("y", "dhp", [], ["hpin"], T.hpin[:], T.hp[:])
    dma("s", "dmt", [], ["mtin"], T.mtin[:], T.mt[:])
    dma("s", "div", [], ["ivin"], T.ivin[:], T.iv[:])
    dma("y", "dx", [], ["xin"], T.xin[:], T.x[:], 4.0)
    dma("y", "du", [], ["uin"], T.uin[:], T.u[:], 4.5)
    dma("s", "dud", [], ["udin"], T.udin[:], T.ud[:], 4.5)
    dma("y", "dws", ["uin"], ["sw_"], T.sw_[:], T.ws[:])
    dma("y", "dwc", ["uin"], ["qw"], T.qw[:].bitcast(dt.uint8), T.wc[:], 4.0)
    dma("y", "dv", ["uin"], ["vin"], T.vin[:], T.v[:], 5.0)

    fl = {"allow_small_or_imprecise_dtypes": True}
    op("iota", 16, [], ["ti"], T.ti[:], [[1, 16]], 128, -1)
    op("iota", 20, [], ["pa"], T.pa[:], [[0, 20]], 0, 1)
    op("iota", C, [], ["iden"], iden, [[1, C]], 0, 0, **fl)
    op("ts", 1, ["ti"], ["ti"], T.ti[:], T.ti[:], 15, None, A.bitwise_and)
    op("ts", 1, ["pa"], ["pa"], T.pa[:], T.pa[:], 15, None, A.bitwise_and)
    op("copy", 1, ["pa"], ["po"], T.po[:], T.pa[:])
    op("ts", 1, ["ti"], ["d48"], T.d48[:, 0:16], T.ti[:], 0.0, LOW, A.is_equal, A.mult)
    op("ts", 1, ["ti"], ["z48"], T.z48[:, 0:16], T.ti[:], 1.0, BIG, A.is_equal, A.mult)
    op("tt", 1, ["d48", "z48"], ["m16"], T.m16[:, 0:16], T.d48[:, 0:16], T.z48[:, 0:16], A.add)
    pick("s", C, ["m16", "po"], ["msk"], T.msk[:], T.m16[:, 0:16], T.po[:])
    op("ts", 1, ["m16"], ["m16s"], T.m16[:, 16:32], T.m16[:, 0:16], BIGS / BIG, None, A.mult)
    pick("s", C, ["m16s", "po"], ["msks"], T.msks[:], T.m16[:, 16:32], T.po[:])
    op("ts", 1, ["pa"], ["big"], big, T.pa[:, 0:1], 15.0, BIG, A.is_lt, A.mult)
    op("ts", 1, ["pa"], ["bigs"], bigs, T.pa[:, 0:1], 15.0, -BIGS, A.is_lt, A.mult)
    op("copy", 1, ["pa"], ["pf"], pf, T.pa[:, 0:1])
    for n in ("hp", "iv", "mt", "ud"):
        op("copy", 1, [n + "in"], [n + "o"], T[n + "o"][:], T[n + "in"][:])
    op("set", 260, [], ["ones"], T.ones[:], 1.0)
    op("sel", 520, ["ones"], ["eb"], T.eb[:], T.ones[:], [[1, 520]], A.is_equal, 0.0, -3, -4)
    for i in range(4):
        quant(128, ["eb"], [("qe", i)], T.qe[:, 128 * i:128 * i + 128], T.se[:, 128 * i:128 * i + 128], T.eb[:, 3 - i:3 - i + 512])
        op("set", 1, [], [("d%d" % i, -1)], T["d%d" % i][:, 0:PADZ], 0)
    op("set", 192, [], ["scs"] + [("scs", k) for k in range(4)], T.scs[:], 0.0)
    op("set", 288, [], [("sc", k) for k in range(1, 5)], T.sc[:], 0.0)
    op("iota", C, [], ["tab"], T.tab[:], [[int(K), C]], 1, 0, **fl)
    op("set", 1, [], ["tab"], T.tab[:, 0:1], K * C)
    op("iota", C, [], ["km"], T.km[:], [[1, C]], -1, 0, **fl)
    op("set", 1, [], ["km"], T.km[:, 0:1], float(C - 1))
    op("set", 1, [], ["rwend"], T.rw[:, C:C + 8], float(C - 1))

    powers = [1, 2, 3, 4, 8, 12, 0, 16, 32, 48]

    def power(e):
        s = powers.index(e % 64 if e != 64 else 1)
        return T.pw[:, C * s:C * s + C]

    def raise_to(e, src, off, turn):
        dst, win = power(e), (iden if src == 0 else power(src))
        s = powers.index(e if e != 64 else 1) * C
        rd, wr = [("pw", src, 0), ("pw", src, 1), off], [("pw", e if e != 64 else 1, h) for h in range(2)]
        if src == 0:
            rd = ["iden", off]
        if turn < CFG["split"]:
            for h, q in enumerate("vs"):
                pick(q, H, rd, [wr[h]], T.pw[:, s + H * h:s + H * h + H], win, T[off][:, 10 * h:10 * h + 10])
        else:
            pick("s", C, rd, wr, dst, win, T[off][:])

    def pk(*es):
        return [("pw", e if e != 64 else 1, h) for e in es for h in range(2)]

    op("iota", C, [], pk(0), power(0), [[1, C]], 0, 0, **fl)
    for turn, (e, src, off) in enumerate(((1, 0, "hpo"), (2, 1, "hpo"), (3, 2, "hpo"), (4, 3, "hpo"), (8, 4, "ro4"), (12, 8, "ro4"), (16, 12, "ro4"),
                                          (32, 16, "ro16"), (48, 32, "ro16"), (64, 48, "ro16"))):
        if e == 64:
            continue
        raise_to(e, src, off, turn)
        if e in (4, 16):
            offsets(C, pk(e), ["ro%d" % e], T["ro%d" % e][:], "rsc", power(e))
    op("ts", 1, ["pa"], ["ci0"], T.ci[:, 0:1], T.pa[:, 0:1], 3, None, A.bitwise_and)
    op("ts", 1, ["ci0"], ["x0"], T.x0[:, 0:1], T.ci[:, 0:1], -float(C), 4.0 * C - 1, A.mult, A.add)
    op("iota", 1, [], ["ci1"], T.ci[:, 2:3], [[0, 1]], 128 + 11, -1)
    op("ts", 1, ["ci1"], ["ci1"], T.ci[:, 2:3], T.ci[:, 2:3], 2, 3, A.logical_shift_right, A.bitwise_and)
    op("ts", 1, ["ci1", "big"], ["slot"], slot, T.ci[:, 2:3], float(C), big, A.mult, A.subtract)
    pick("s", 16, pk(1, 2, 3, 4) + ["x0"], ["wl"], T.wl[:], T.pw[:, 0:4 * C], T.x0[:, 0:1])
    offsets(16, ["wl"], ["x1"], T.x1[:, 0:1], "sb", T.wl[:], ("slot", slot))
    pick("s", 16, pk(4, 8, 12, 0) + ["x1"], [("rw", 19)], T.rw[:, C - 16:C], T.pw[:, 3 * C:7 * C], T.x1[:, 0:1])
    offsets(16, [("rw", 19)], ["lo"], T.lo[:, 0:1], "sb", T.rw[:, C - 16:C])
    for e in (16, 32, 48):
        pick("s", 16, pk(e) + ["lo"], [("rw", 19 - e // 16)], T.rw[:, C - 16 - e:C - e], power(e), T.lo[:, 0:1])
    raise_to(64, 48, "ro16", 9)
    offsets(64, [("rw", c) for c in range(16, 20)], [("ro", 4)], T.ro[:, 16:20], "sb", T.rw[:, C - 64:C])
    for k in (3, 2, 1, 0):
        pick("s", 64, pk(64) + [("ro", k + 1)], [("rw", k)], T.rw[:, 64 * k:64 * k + 64], power(64), T.ro[:, 4 * k + 4:4 * k + 8])
        offsets(64, [("rw", k)], [("ro", k)], T.ro[:, 4 * k:4 * k + 4], "sb", T.rw[:, 64 * k:64 * k + 64])
    ro, rw = [("ro", k) for k in range(5)], [("rw", k) for k in (0, 1, 2, 3, 16, 17, 18, 19)]
    op("ts", 1, ro, ["ordo"], T.ordo[:], T.ro[:], -1.0, float(PADZ + C - 1), A.mult, A.add)
    op("tt", C, rw + ["rwend"], ["wd"], T.wd[:], T.rw[:, 0:C], T.rw[:, 1:C + 1], A.subtract)
    op("copy", C, ro + ["km"], ["pm"], T.pm[:].indirect(T.ro[:]), T.km[:], kind="scatter")
    offsets(C, ["pm"], ["pmo"], T.pmo[:], "rsc", T.pm[:])

    pick("s", C, ["iden", "mto"], ["mtw"], T.mtw[:], iden, T.mto[:])
    pick("s", C, ["iden", "ivo"], ["aw"], T.aw[:], iden, T.ivo[:])
    pick("s", C, ["mtw", "ivo"], ["bw0"], T.bw0[:], T.mtw[:], T.ivo[:])
    op("set", 768, [], ["sab"], T.sab[:], 0.0)
    for n, w in enumerate(("aw", "bw0")):
        for k in range(4):
            scan(80, [w, "sab"], [("sab", n, k)], T.sab[:, 384 * n + 96 * k:384 * n + 96 * k + 80], T[w][:, 3 - k::4])
    op("iota", 48, [], ["jj"], T.jj[:], [[0, 2], [-1, 4], [64, 6]], 3, 0, **fl)
    op("iota", 48, [], ["pp"], T.pp[:], [[0, 2], [80, 4], [16, 6]], PADZ, 0, **fl)
    op("ts", 1, ["pf", "big"], ["jb"], T.col[:, 4:5], pf, 4.0, big, A.mult, A.add)
    op("ts", 1, ["jj", "jb"], ["jj"], T.jj[:], T.jj[:], T.col[:, 4:5], None, A.add)
    op("ts", 1, ["pp", "pf"], ["pp"], T.pp[:], T.pp[:], pf, None, A.add)
    op("tt", 1, [("sab", n, k) for n in range(2) for k in range(4)] + ["jj"], ["d48"], T.d48[:], T.sab[:, 15::16], T.jj[:], A.subtract)
    op("ts", 1, ["d48"], ["z48"], T.z48[:], T.d48[:], -4.0, 4.0, A.mult, A.add)
    op("ts", 1, ["d48"], ["w48"], T.w48[:], T.d48[:], 0.0, None, A.max)
    op("tt", 1, ["d48", "z48"], ["z48"], T.z48[:], T.z48[:], T.d48[:], A.max)
    op("ts", 1, ["z48"], ["z48"], T.z48[:], T.z48[:], -80.0, None, A.mult)
    op("tt", 1, ["z48", "pp"], ["z48"], T.z48[:], T.z48[:], T.pp[:], A.add)

    def both(p, rd, a, b):
        op("tt", 1, rd, [("mid", p)], part("mid", p), a, b, A.add)
        op("tt", 1, rd, [("dif", p)], part("dif", p), b, a, A.subtract)
        centre(p, [p], rd, a)

    def centre(p, ks, rd, now):
        n = (p[1] - p[0]) // 2
        op("ts", 2 * n, [("dif", k) for k in ks] + ["bigs"], [("cen", k) for k in ks], part("cen", p), part("dif", p), bigs, None, A.mult)
        op("tt", n, [("cen", k) for k in ks] + rd, [("cen", k) for k in ks], part("cen", p), part("cen", p), now, A.add)

    both(DI, ["w48"], T.w48[:, 0:24], T.w48[:, 24:48])
    both(OF, ["z48"], T.z48[:, 0:24], T.z48[:, 24:48])
    offsets(C, ["bw0"], ["t20"], T.t20[:], "se_", T.bw0[:])
    both(IV, ["ivin", "t20"], T.ivin[:], T.t20[:])
    pick("s", C, ["iden", "udo"], ["uw"], T.uw[:], iden, T.udo[:])
    pick("s", C, ["uw", "mto"], ["umw"], T.umw[:], T.uw[:], T.mto[:])
    offsets(C, ["umw"], ["t20"], T.t20[:], "se_", T.umw[:])
    both(UD, ["udin", "t20"], T.udin[:], T.t20[:])
    KK = [None, (0, 18), (18, 36), (36, 52)]
    op("iota", 36, [], ["kk"], T.kk[:, 0:36], [[0, 2], [80, 3], [16, 6]], PADZ + 80, 0, **fl)
    op("iota", 16, [], ["kk3"], T.kk[:, 36:52], [[16, 16]], PADZ + 64, 0, **fl)
    op("ts", 1, ["kk", "kk3", "pf"], ["kk", "kk3"], T.kk[:, 0:52], T.kk[:, 0:52], pf, 0.25, A.add, A.add)
    for s in (1, 2, 3):
        op("ts", 1, ["kk", "kk3", "big"], [("kk", s)], part("kk", KK[s]), part("kk", KK[s]), -K * SIZES[s] / C, big, A.mult, A.subtract)

    quant(C, ["xin"], ["qx0"], T.qx0[:], T.sx0[:], T.xin[:])
    quant(128, ["uin"], ["qu"], T.qu[:], T.su[:], T.uin[:])
    op("iota", 8, [], ["c8"], T.c8[:], [[16, 8]], 0, 0)
    op("copy", 1, ["c8"], ["uof"], T.uof[:], T.c8[:])
    op("copy", 128, ["qu", "uof"], ["qr"], T.qr[:].bitcast(dt.uint32), T.qu[:].bitcast(dt.uint32).indirect(T.uof[:]), kind="gather")
    pick("s", 128, ["qu", "uof"], ["sr"], T.sr[:], T.su[:], T.uof[:])
    quant(128, ["vin"], ["qv"], T.qv_[:], T.sv[:], T.vin[:])

    OWNB, PARB = [1, 2, 3, 4], [5, 6, 7, 0]

    def unpack(dst, banks, qn, sn, rd):
        for i in range(4):
            mm(banks[i], C, [("qe", i)] + rd, T.qe[:, 128 * i:128 * i + 128], T.se[:, 128 * i:128 * i + 128], T[qn][:], T[sn][:])
            op("act", C, ["ps%d" % banks[i]], [(dst, i)], T[dst][:, C * i:C * i + C], T["ps%d" % banks[i]][:, 0:C], F.Copy, scale=0.5)

    def edit(r, ps, views):
        lst, whole = "lst%d" % r, (ps[0][0], ps[-1][1])
        for p, (rd, v) in zip(ps, views):
            op("tt", 1, rd + [("dif", p)], [("mul", p)], part("mul", p), v, part("dif", p), A.mult)
        op("tt", 24 * len(ps), [(n, p) for n in ("mul", "cen") for p in ps], [("val", p) for p in ps], part("val", whole), part("mul", whole), part("cen", whole), A.add)
        op("copy", 1, [("val", p) for p in ps], [(lst, p) for p in ps], part(lst, whole), part("val", whole))

    def stage(s, off, offk, cols, src, srck):
        w, d = C // RAD[s], T["d%d" % s]
        for k in range(1, RAD[s]):
            lim, c0 = PADZ + k * w, cols * (k - 1)
            op("tt", w, [("d%d" % s, i) for i in range(-1, k)] + [offk] + srck(k), [("d%d" % s, k)], d[:, lim:lim + w],
               d[:, 0:lim].indirect(off[:, c0:c0 + w // 16] if s else T[off[0]][:, off[1] + c0:off[1] + c0 + w // 16]), src(k), A.add, kind="gather")

    for r in range(3):
        qx, sx, qp, sp, lst = "qx%d" % r, "sx%d" % r, "qp%d" % r, "sp%d" % r, "lst%d" % r
        ivp, bn, bp, en, ep = ["%s%d" % (n, r) for n in ("ivp", "bn", "bp", "en", "ep")]
        send(r, [qx], qp, T[qp][:].bitcast(dt.uint8), T[qx][:].bitcast(dt.uint8), "aq%d" % r, 4.0)
        send(r, [qx], sp, T[sp][:], T[sx][:], "as%d" % r, 5.0)
        mm(0, C, ["qr", "sr", qx], T.qr[:], T.sr[:], T[qx][:], T[sx][:])
        op("ts", C, ["ps0"], ["np"], T.np_[:], T.ps0[:, 0:C], 0.0, None, A.is_le)
        for h in range(2):
            a = H * h
            mm(5 + h, H, ["qr", "sr", qx], T.qr[:], T.sr[:], T[qx][:, a:a + H], T[sx][:, a:a + H])
            op("act", H, ["ps%d" % (5 + h)], [("sg", h)], T.sg[:, a:a + H], T["ps%d" % (5 + h)][:, 0:H], F.Sign)
            op("tt", H, ["np", ("sg", h), "mto"], [("sw", h)], T.sw[:, a:a + H], T.np_[:].indirect(T.mto[:, 10 * h:10 * h + 10]), T.sg[:, a:a + H], A.is_lt, kind="gather")
        sw = [("sw", 0), ("sw", 1)]
        for h, q in enumerate("vs"):
            pick(q, H, sw + ["ivo"], [("sa", h)], T.sa[:, H * h:H * h + H], T.sw[:], T.ivo[:, 10 * h:10 * h + 10])
        sa = [("sa", 0), ("sa", 1)]
        for k in range(4):
            scans(80, sa, [("scs", k)], T.scs[:, 96 * k:96 * k + 80], T.sa[:, 3 - k::4])
        edit(r, [DI, OF], [([("scs", k) for k in range(4)], T.scs[:, 15::16])] * 2)
        scans(C, sa, [("scn", 0)], T.scn[:, 0:C], T.sa[:])
        scans(C, sw, [("scn", 1)], T.scn[:, C:2 * C], T.sw[:])
        edit(r, [IV], [([("scn", 0)], T.scn[:, 15:C:16])])
        edit(r, [UD], [([("scn", 1)], T.scn[:, C + 15::16])])
        send(r, [(lst, IV)], ivp, li(ivp), part(lst, IV), "ai%d" % r)
        if r < 2:
            ps = [DI, OF, IV, UD]
            op("ts", 88, [("val", p) for p in ps], [("dif", p) for p in ps], T.dif[:], T.val[:], -2.0, None, A.mult)
            op("tt", 88, [(n, p) for n in ("dif", "mid") for p in ps], [("dif", p) for p in ps], T.dif[:], T.dif[:], T.mid[:], A.add)
            centre(ALL, ps, [("val", p) for p in ps], T.val[:])
        unpack("th", OWNB, qx, sx, [qx])
        for k, q in enumerate("svss"):
            out, key = (T.d0[:, PADZ:PADZ + 80], ("d0", 0)) if k == 0 else (T.e0[:, 80 * k:80 * k + 80], ("e0", k))
            pick(q, 80, ["tab", (lst, DI)], [key], out, T.tab[:], T[lst][:, 6 * k:6 * k + 5])
        stage(0, (lst, OF[0] + 6), (lst, OF), 6, lambda k: T.e0[:, 80 * k:80 * k + 80], lambda k: [("e0", k)])
        for s in (1, 2, 3):
            q, was = RAD[s], "d%d" % (s - 1)
            w, ks = C // q, [(was, i) for i in range(RAD[s - 1])]
            cols = 6 if w == 80 else 4

            def view(k, q=q, was=was):
                return T[was][:, PADZ + q - 1 - k:PADZ + C:q]
            for k in range(1, q):
                scan(w, ks, [("sc", k)], T.sc[:, 16 * cols * (k - 1):16 * cols * (k - 1) + w], view(k))
            n = cols * (q - 1)
            op("tt", 1, [("sc", k) for k in range(1, 5)] + [("kk", s)], ["t1"], T.t1[:, 0:n], T.sc[:, 15:16 * n:16], part("kk", KK[s]), A.add)
            op("copy", w, ks, [("d%d" % s, 0)], T["d%d" % s][:, PADZ:PADZ + w], view(0))
            op("ts", 1, ["t1"], ["oa"], T.oa[:, 0:n], T.t1[:, 0:n], -C / SIZES[s] / K, None, A.mult)
            stage(s, T.oa, "oa", cols, view, lambda k, ks=ks: ks)
        unpack("thp", PARB, qp, sp, [qp, sp])
        for i in range(4):
            pick("s", C, [("thp", i), ivp], [("tiv", i)], T.tiv[:, C * i:C * i + C], T.thp[:, C * i:C * i + C], li(ivp))
        op("ts", C, [("d3", i) for i in range(-1, 5)] + ["ordo"], ["ne"], T.ne[:], T.d3[:].indirect(T.ordo[:]), 1, None, A.bitwise_and, kind="gather")
        op("scan", C, ["ne", "wd"], ["st"], T.st[:], T.ne[:], T.wd[:], 0.0, A.mult, A.add)
        for h in range(2):
            a, c = H * h, 10 * h
            op("tt", H, ["st", "pmo", "iden"], [("bw", h)], T.bw[:, a:a + H], T.st[:].indirect(T.pmo[:, c:c + 10]), T.iden[:, a:a + H], A.add, kind="gather")
            offsets(H, [("bw", h)], [(bn, h)], li(bn, c, 10), ("sb", "rsc")[h], T.bw[:, a:a + H])
            send(r, [(bn, h)], (bp, h), li(bp, c, 10), li(bn, c, 10), ("ab%d", "ac%d")[h] % r)
        pick("s", C, [("bw", 0), ("bw", 1), ivp], ["ew"], T.ew[:], T.bw[:], li(ivp))
        offsets(C, ["ew"], [en], li(en), "se_", T.ew[:])
        send(r, [en], ep, li(ep), li(en), "ae%d" % r)
        for i in range(4):
            pick("s", C, [("th", i), (lst, UD)], [("tu", i)], T.tu[:, C * i:C * i + C], T.th[:, C * i:C * i + C], part(lst, UD))
        if r == 2:
            pick("s", C, ["iden", (lst, UD)], ["uw"], T.uw[:], iden, part(lst, UD))
            dma("y", "duo", ["uw"], [], T.uo[:, :], T.uw[0:128:16, :])
        for h in range(2):
            a, c = H * h, 10 * h
            for i in range(4):
                op("tt", H, [("thp", i), ("tiv", i), (bp, h)], [("zt", h, i)], T.zt[:, 4 * a + i:4 * a + 4 * H:4],
                   T.thp[:, C * i:C * i + C].indirect(li(bp, c, 10)), T.tiv[:, C * i + a:C * i + a + H], A.add, kind="gather")
            quant(H, [("zt", h, i) for i in range(4)], [("qz", h)], T.qz[:, a:a + H], T.sz[:, a:a + H], T.zt[:, 4 * a:4 * a + 4 * H])
            for i in range(4):
                bank = (OWNB, PARB)[h][i]
                mm(bank, H, ["qw", "sw_", ("qz", h)], T.qw[:, 128 * i:128 * i + 128], T.sw_[:, 128 * i:128 * i + 128], T.qz[:, a:a + H], T.sz[:, a:a + H])
                op("act", H, ["ps%d" % bank], [("hh", i, h)], T.hh[:, C * i + a:C * i + a + H], T["ps%d" % bank][:, 0:H], F.Copy, scale=2.0 ** -6)
        qn, sn = "qx%d" % (r + 1), "sx%d" % (r + 1)
        for h, (a, n) in enumerate(((0, C),) if r < 2 else ((0, H), (H, H))):
            for i in range(4):
                op("tt", n, [("hh", i, 0), ("hh", i, 1), ("tu", i), ep], [("xt", i, h)] + ([("xt", i, 1)] if n == C else []), T.xt[:, 4 * a + i:4 * (a + n):4],
                   T.hh[:, C * i:C * i + C].indirect(li(ep, a // 16, n // 16)), T.tu[:, C * i + a:C * i + a + n], A.add, kind="gather")
            key = qn if r < 2 else (qn, h)
            quant(n, [("xt", i, h) for i in range(4)], [key], T[qn][:, a:a + n], T[sn][:, a:a + n], T.xt[:, 4 * a:4 * (a + n)])
            if r == 2:
                dma("y", "doc%d" % h, [key], [], T.oc[:, 4 * a:4 * (a + n)], T[qn][:, a:a + n].bitcast(dt.uint8), 2.5)
                mm(1 + h, n, ["qv", key], T.qv_[:], T.sv[:], T[qn][:, a:a + n], T[sn][:, a:a + n])
                op("act", n, ["ps%d" % (1 + h)], [("ys", h)], T.ys[:, a:a + n], T["ps%d" % (1 + h)][:, 0:n], F.Copy)
                dma("s", "dy%d" % h, [("ys", h)], [], T.y[:, a:a + n], T.ys[:, a:a + n], 2.5)
    for k in range(4):
        dma("y", "ds%d" % k, [("qx3", 0), ("qx3", 1)], [], T.osc[4 * k:4 * k + 4, :], T.sx3[32 * k:32 * k + 4, :])

    token, seen = {}, {q: {} for q in eng}
    for i in order(calls):
        q, need = calls[i]["q"], {}
        for d in calls[i]["deps"]:
            s, n = token[d]
            need[s] = max(need.get(s, 0), n)
        for s, n in need.items():
            if seen[q].get(s, 0) < n:
                eng[q].wait_ge(T.sem[s], n)
                seen[q][s] = n
        token[i] = calls[i]["issue"]()
    for s, n in count.items():
        g.wait_ge(T.sem[s], n)
